import numpy as np, ml_dtypes
CORES = [3,11,19,27,35,43,51,59]
N = 8
BF = ml_dtypes.bfloat16
def gentries(a):
    return np.ascontiguousarray(a.reshape(8, 16, -1).transpose(0, 2, 1)).reshape(8, -1)
def gtable(e):
    e = np.asarray(e); return np.ascontiguousarray(e.reshape(8, -1, 16).transpose(0, 2, 1)).reshape(128, -1).astype(np.int32)
I, W, PL, RO, CNT, B, AS = 192, 3072, 2048, 8, 12, 24, 64
def records(x, s):
    return np.take_along_axis(x, s.transpose(0, 1, 3, 2).reshape(N, 8, 1, 16 * I), 3).reshape(N, 8, 16, I, 16)
def dist(xs, z):
    return np.sum(np.abs(xs - z[..., None]), axis=2).transpose(0, 1, 3, 2)
def parts(rng):
    x = (256 * rng.random((N, 8, 16, W)) * rng.choice(np.array([1.0, 1.0, 0.5, 0.25]), (N, 8, 1, W))).astype(np.int64)
    z = rng.integers(0, 256, (N, 8, 16, I)); f = rng.integers(0, 256, (N, 8, 16, I))
    s = rng.integers(0, W, (N, 8, 16, I)); pl = rng.integers(0, W, (N, 8, 16, PL)); p = rng.integers(0, PL, (N, 8, I))
    th = rng.integers(300, 1300, (N, 8, 1, I)) + rng.integers(0, 200, (N, 8, 16, I))
    return x, z, f, s, pl, p, th
def pack(x, z, f, s, pl, p, th):
    return {"x0": x.reshape(N, 128, W).astype(np.float32).astype(BF), "z0": z.reshape(N, 128, I).astype(np.float32).astype(BF), "f0": f.reshape(N, 128, I).astype(np.float32).astype(BF),
            "s0": s.reshape(N, 128, I).astype(np.int32), "pl": pl.reshape(N, 128, PL).astype(np.int32), "p0": np.stack([gtable(a) for a in p]), "th": th.reshape(N, 128, I).astype(np.int32)}
def setup_inputs(rng):
    return pack(*parts(rng))
def setup_inputs_spread(rng):
    x = (np.exp2(8 * rng.random((N, 8, 1, W))) * rng.random((N, 8, 16, W))).astype(np.int64)
    z = (np.exp2(8 * rng.random((N, 8, 1, I))) * rng.random((N, 8, 16, I))).astype(np.int64)
    f = (np.exp2(8 * rng.random((N, 8, 1, I))) * rng.random((N, 8, 16, I))).astype(np.int64)
    s = (W * rng.random((N, 8, 16, I)) ** 3).astype(np.int64); pl = (W * rng.random((N, 8, 16, PL)) ** 2).astype(np.int64); p = (PL * rng.random((N, 8, I)) ** 3).astype(np.int64)
    th = np.minimum((np.exp2(5 + 7 * rng.random((N, 8, 1, I))) * (0.5 + 0.5 * rng.random((N, 8, 16, I)))).astype(np.int64), 4080)
    return pack(np.minimum(x, 255), np.minimum(z, 255), np.minimum(f, 255), np.minimum(s, W - 1), np.minimum(pl, W - 1), np.minimum(p, PL - 1), th)
def setup_inputs_ends(rng):
    def mix(n):
        return np.where(rng.random((N, 8, 1, n)) < 0.5, rng.integers(0, 2, (N, 8, 16, n)), rng.integers(0, 2, (N, 8, 1, n)))
    x = 255 * mix(W); z = 255 * mix(I); f = 255 * mix(I); th = 4080 * mix(I)
    s = (W - 1) * rng.integers(0, 2, (N, 8, 16, I)); pl = (W - 1) * rng.integers(0, 2, (N, 8, 16, PL)); p = (PL - 1) * rng.integers(0, 2, (N, 8, I))
    x[:, 1::2, :, W - 1] = 255; x[:, 1::2, :, 0] = 0; x[:, 0:4:2, :, W - 1] = 0; x[:, 0:4:2, :, 0] = 255
    pl[:, 7, :, PL - 1] = W - 1; pl[:, 7, :, 0] = 0; pl[:, 7, 0, 768] = 0
    for i in (0, 1, I - 2, I - 1):
        z[:, 7, :, i] = 0; f[:, 7, :, i] = 0; s[:, 7, :, i] = W - 1; th[:, 7, :, i] = 4080; p[:, 7, i] = PL - 1
    for i in (2, 3, I - 4, I - 3):
        z[:, 7, :, i] = 255; f[:, 7, :, i] = 255; s[:, 7, :, i] = 0; th[:, 7, :, i] = 4080; p[:, 7, i] = 0
    return pack(x, z, f, s, pl, p, th)
def setup_inputs_ties(rng):
    x, z, f, s, pl, p, th = parts(rng)
    x = 64 * rng.integers(0, 4, (N, 8, 16, W)); z = 64 * rng.integers(0, 4, (N, 8, 16, I))
    few = np.take_along_axis(rng.integers(0, W, (N, 8, 3, I)), rng.integers(0, 3, (N, 8, 16, I)), 2)
    s = np.where(rng.random((N, 8, 1, I)) < 0.5, few, s)
    ds = dist(records(x, s), z); dp = dist(records(x, np.take_along_axis(pl, p[:, :, None, :], 3)), z)
    one = (rng.random((N, 8, 16, I)) < 0.08).astype(np.int64); k = rng.integers(0, 3, (N, 8, 1, I))
    th = np.where(k == 0, ds + one, np.where(k == 1, np.minimum(dp + one, ds), np.minimum(dp, ds)))
    return pack(x, z, f, s, pl, p, np.minimum(th, 4080))
def setup_inputs_odd(rng):
    x, z, f, s, pl, p, th = parts(rng); h = W // 2
    o = np.argsort(rng.random((N, 8, W)), axis=-1)
    hi = np.zeros((N, 8, W), np.int64); np.put_along_axis(hi, o[:, :, h:], 1, 2)
    x = rng.integers(0, 56, (N, 8, 16, W)) + 200 * hi[:, :, None, :]; x[:, :, 15] ^= np.sum(x, axis=2) & 1
    kz = rng.integers(0, 2, (N, 8, 1, I)); z = rng.integers(0, 56, (N, 8, 16, I)) + 200 * kz; z[:, :, 15] ^= (np.sum(z, axis=2) & 1) ^ 1
    s = np.take_along_axis(o, (rng.integers(0, h, (N, 8, 16, I)) + h * (1 - kz)).reshape(N, 8, 16 * I), 2).reshape(N, 8, 16, I)
    pl = np.take_along_axis(o, (rng.integers(0, h, (N, 8, 16, PL)) + h * (np.arange(PL) & 1)).reshape(N, 8, 16 * PL), 2).reshape(N, 8, 16, PL)
    p = 2 * rng.integers(0, PL // 2, (N, 8, I)) + 1 - kz[:, :, 0]
    x[:, :, :, W - 1] = 255; x[:, ::2, :, W - 3] = 0; x[:, 1::2, :, 1] = 0
    pl[:, :, 0, PL - 1] = W - 1; pl[:, ::2, 0, 0] = W - 3; pl[:, 1::2, 0, 0] = 1
    ds = dist(records(x, s), z); dp = dist(records(x, np.take_along_axis(pl, p[:, :, None, :], 3)), z)
    one = (rng.random((N, 8, 16, I)) < 0.08).astype(np.int64); k = rng.integers(0, 3, (N, 8, 1, I))
    th = np.where(k == 0, ds + one, np.where(k == 1, np.minimum(dp + one, ds), np.minimum(dp, ds)))
    th = np.minimum(th, 4080)
    for i in (0, 1, I - 2, I - 1):
        z[:, :, :, i] = 0; f[:, :, :, i] = 0; s[:, :, 0, i] = W - 1; p[:, :, i] = PL - 1; th[:, :, :, i] = 0; th[:, :, 0, i] = 4080
    return pack(x, z, f, s, pl, p, th)
def setup_inputs_corners(rng):
    x, z, f, s, pl, p, th = parts(rng)
    k = rng.integers(0, 8, (N, 8, I)); k[:, :, I - 8:] = np.arange(8); k = k[:, :, None, :]; row = np.arange(16)[:, None]
    th = 4080 * ((((k == 1) | (k == 4) | (k == 5)) & (row == 15)) | ((k == 2) & (row == 0)) | (k == 3)).astype(np.int64)
    th = np.where(k == 7, rng.integers(0, 4081, (N, 8, 16, I)), th)
    z = np.where(k == 4, 255, np.where((k == 5) | (k == 7) | ((k == 0) & (rng.random((N, 8, 1, I)) < 0.5)), 0, z))
    z = np.where(k == 6, np.where(row == 1, 100, 15), z)
    s = np.where(k == 2, (W - 1) * rng.integers(0, 2, s.shape), s); s = np.where(k == 3, rng.integers(0, W, (N, 8, 1, I)), s)
    s = np.where(k == 7, 16 * np.arange(I) + rng.integers(0, 16, s.shape), s); s = np.where((k == 5) & (row == 15), W - 1, s)
    x[:, :, :, W - 1] = 255
    pl[:, :, :, 0] = rng.integers(0, W - 1, (N, 8, 1)); pl[:, :, :, PL - 1] = W - 1; pl[:, :, 15, :] = rng.integers(0, W - 1, (N, 8, PL))
    e = rng.integers(0, 4, (N, 8, I)); p = np.where(e == 0, 0, np.where(e == 1, PL - 1, p))
    return pack(x, z, f, s, pl, p, th)
def check_inputs(d):
    bad = []
    for k, lo, hi in (("x0", 0, 255), ("z0", 0, 255), ("f0", 0, 255), ("s0", 0, W - 1), ("pl", 0, W - 1), ("p0", 0, PL - 1), ("th", 0, 4080)):
        v = np.asarray(d[k]).astype(np.float64)
        if not np.all((v >= lo) & (v <= hi) & (v == np.floor(v))): bad.append("range of " + k)
    return bad
def reference(x0, z0, f0, s0, pl, p0, th):
    X = x0.astype(np.float32).astype(np.int32).reshape(N, 8, 16, W); z = z0.astype(np.float32).astype(np.int32).reshape(N, 8, 16, I); f = f0.astype(np.float32).astype(np.int32).reshape(N, 8, 16, I)
    S = s0.astype(np.int32).reshape(N, 8, 16, I); plans = pl.astype(np.int32).reshape(N, 8, 16, PL); lim = th.astype(np.int32).reshape(N, 8, 16, I)
    P = np.stack([gentries(a) for a in p0]).astype(np.int32); A = np.zeros((N, 8, I), np.int32)
    row = np.arange(16)[:, None]; wt = (2 * np.arange(16) + 1)[:, None]
    for t in range(RO):
        e = np.take_along_axis(plans, P[:, :, None, :], 3)
        xs = records(X, S); xe = records(X, e); bound = lim + AS * A[:, :, None, :]
        rs = dist(xs, z) < bound; rp = dist(xe, z) < bound
        c1 = np.any(rs, axis=2); c2 = ~c1 & np.any(rp, axis=2); c3 = ~c1 & ~c2
        j = np.argmax(rs, axis=2); jp = np.argmax(rp, axis=2)
        u = np.sum(wt * z, axis=2) & 4095; A = A + c3; P = np.where(c3, ((u * u >> 5) + 37 * u) & (PL - 1), P).astype(np.int32)
        low = np.sum(xs <= z[..., None], axis=2).transpose(0, 1, 3, 2)
        R = np.where(c1[:, :, None, :] & (low >= CNT) & (row != j[:, :, None, :]), e, S)
        t1 = np.take_along_axis(S, j[:, :, None, :], 2)[:, :, 0]; t2 = np.take_along_axis(e, jp[:, :, None, :], 2)[:, :, 0]; t3 = np.take_along_axis(plans[:, :, 0], P, 2)
        top = np.where(c1, t1, np.where(c2, t2, t3)); last = np.where(c1, j, 15)
        S = np.where(row <= last[:, :, None, :], np.concatenate([top[:, :, None, :], R[:, :, :15]], axis=2), R).astype(np.int32)
        f = (f + z) >> 1
        y = np.abs(np.take_along_axis(X, S[:, :, :1, :], 3) - f)
        place = 16 * np.arange(I) + (np.sum(y, axis=2) & 15)
        np.put_along_axis(X, place[:, :, None, :], (y + z) >> 1, 3)
        if t < RO - 1:
            z = np.concatenate([np.roll(y[..., b * B:(b + 1) * B], b + t, axis=0) for b in range(N)], axis=3)
    yx = np.sum(X.reshape(N, 8, 16, I, 16) * np.arange(1, 17), axis=4)
    return {"ys": S.reshape(N, 128, I).astype(np.float32), "yp": np.stack([gtable(a) for a in P + PL * A]).astype(np.float32),
            "yf": f.reshape(N, 128, I).astype(np.float32).astype(BF), "yx": yx.reshape(N, 128, I).astype(np.float32)}

@@ -1,0 +1,539 @@
+import numpy as np
+from concourse.bass import DstId, RemoteDMATransfer
+from concourse.mybir import dt, AluOpType, AxisListType, ActivationFunctionType
+
+A = AluOpType
+F = ActivationFunctionType
+I, W, PLN, TURNS, BLK, N = 192, 3072, 2048, 8, 24, 8
+NK = 2
+NQ = 1
+NF = 0
+NC = 16 // NK
+CW = NK * I
+CEN = 1536.0
+MAGIC = 12582912.0
+MAGIC16 = 201326592.0
+
+SCRATCH = {
+    "X": ("sbuf", [128, W], "bfloat16"),
+    "XS": ("sbuf", [128, W], "bfloat16"), "XE": ("sbuf", [128, W], "bfloat16"),
+    "D": ("sbuf", [128, W], "bfloat16"), "AB": ("sbuf", [128, W], "bfloat16"),
+    "SG": ("sbuf", [128, W], "bfloat16"), "MX": ("sbuf", [128, W], "bfloat16"),
+    "PLT": ("sbuf", [128, PLN], "int32"), "SI": ("sbuf", [128, I], "int32"), "THI": ("sbuf", [128, I], "int32"),
+    "PI": ("sbuf", [128, 12], "int32"), "PF": ("sbuf", [128, 12], "float32"),
+    "BND": ("sbuf", [128, I], "float32"), "C64": ("sbuf", [128, I], "float32"), "KK": ("sbuf", [128, I], "float32"),
+    "RS": ("sbuf", [128, I], "bfloat16"), "RP": ("sbuf", [128, I], "bfloat16"), "FI": ("sbuf", [128, I], "bfloat16"),
+    "CR": ("sbuf", [128, I], "bfloat16"), "DES": ("sbuf", [128, I], "float32"), "WD": ("sbuf", [128, I], "float32"),
+    "RR": ("sbuf", [128, I], "float16"), "QQ": ("sbuf", [128, I], "float16"), "FF": ("sbuf", [128, I], "float16"),
+    "GG": ("sbuf", [128, I], "float16"), "HH": ("sbuf", [128, I], "float16"), "HF": ("sbuf", [128, I], "float16"),
+    "E16": ("sbuf", [128, I], "float16"), "CAND": ("sbuf", [128, I], "float16"),
+    "SU": ("sbuf", [128, I], "uint16"), "EU": ("sbuf", [128, I], "uint16"),
+    "TU": ("sbuf", [128, 12], "uint16"), "PU": ("sbuf", [128, 12], "uint16"), "MU": ("sbuf", [128, 12], "uint16"),
+    "FA": ("sbuf", [128, I], "bfloat16"), "FB": ("sbuf", [128, I], "bfloat16"),
+    "YD": ("sbuf", [128, I], "bfloat16"), "WR": ("sbuf", [128, I], "bfloat16"),
+    "H1": ("sbuf", [128, 12], "int32"), "H2": ("sbuf", [128, 12], "int32"), "H3": ("sbuf", [128, 12], "int32"),
+    "H4": ("sbuf", [128, 12], "int32"),
+    "H7": ("sbuf", [128, 12], "int32"), "DP": ("sbuf", [128, 12], "float32"), "DQ": ("sbuf", [128, 12], "float32"),
+    "QF": ("sbuf", [128, 12], "float32"), "RF": ("sbuf", [128, 12], "float32"), "MF": ("sbuf", [128, 12], "float32"),
+    "YPF": ("sbuf", [128, 12], "float32"),
+    "ip": ("sbuf", [128, 1], "int32"), "ig": ("sbuf", [128, 1], "int32"), "irow": ("sbuf", [128, 144], "int32"),
+    "igrow": ("sbuf", [128, 128], "int32"), "ibase": ("sbuf", [128, 12], "int32"),
+    "pf": ("sbuf", [128, 1], "float32"), "p1": ("sbuf", [128, 1], "float32"), "gf": ("sbuf", [128, 1], "float32"),
+    "g16": ("sbuf", [128, 1], "float32"), "g15": ("sbuf", [128, 1], "float32"), "lf": ("sbuf", [128, 1], "float32"),
+    "l21": ("sbuf", [128, 1], "float32"), "l0": ("sbuf", [128, 1], "float32"), "nl0": ("sbuf", [128, 1], "float32"),
+    "nl15": ("sbuf", [128, 1], "float32"), "r16": ("sbuf", [128, 1], "float32"),
+    "row": ("sbuf", [128, 144], "float32"), "grow": ("sbuf", [128, 128], "float32"), "base": ("sbuf", [128, 12], "float32"),
+    "W1": ("sbuf", [128, 144], "bfloat16"), "W2": ("sbuf", [128, 144], "bfloat16"), "Wm": ("sbuf", [128, 144], "bfloat16"),
+    "Wu": ("sbuf", [128, 144], "bfloat16"), "Wh": ("sbuf", [128, 144], "float16"),
+    "OB": ("sbuf", [128, 128], "bfloat16"), "OBm": ("sbuf", [128, 128], "bfloat16"), "Ib": ("sbuf", [128, 128], "bfloat16"),
+    "Im": ("sbuf", [128, 128], "bfloat16"), "im8": ("sbuf", [128, 128], "int32"), "mk": ("sbuf", [128, 128], "float32"),
+    "Ihf": ("sbuf", [128, 128], "bfloat16"), "I100": ("sbuf", [128, 128], "bfloat16"), "GT": ("sbuf", [128, 128], "bfloat16"),
+    "Ls": ("sbuf", [128, 128], "bfloat16"), "Li": ("sbuf", [128, 128], "bfloat16"),
+    "Ih": ("sbuf", [128, 128], "float16"), "Sh": ("sbuf", [128, 128], "float16"),
+    "ShI": ("sbuf", [128, 128], "float16"), "Tp": ("sbuf", [128, 128], "float16"), "TpI": ("sbuf", [128, 128], "float16"),
+    "cq": ("sbuf", [128, I], "bfloat16"), "c75": ("sbuf", [128, 16], "bfloat16"),
+    "IC": ("sbuf", [128, 16 * 128], "bfloat16"),
+    "OS": ("sbuf", [128, I], "float32"), "OX": ("sbuf", [128, I], "float32"),
+}
+for _t in range(8):
+    SCRATCH["L%d" % _t] = ("sbuf", [128, I], "bfloat16")
+    SCRATCH["Y%d" % _t] = ("sbuf", [128, I], "bfloat16")
+for _t in range(8):
+    SCRATCH["b%d" % _t] = ("psum", [128, 512], "float32")
+NDMA = 12
+SEMAPHORES = ["qV", "qS", "qT", "qG", "sent"] + ["arr%d" % t for t in range(8)] + ["dm%d" % k for k in range(NDMA)]
+
+LAT = 0.08
+BONUS = {}
+
+
+def _build():
+    ops = []
+
+    def add(q, fn, rd, wr, cost, **kw):
+        ops.append([q, fn, [(r if len(r) == 3 else (r[0], 0, 1 << 20)) for r in rd], [(r if len(r) == 3 else (r[0], 0, 1 << 20)) for r in wr], cost, kw])
+
+    def al(*names):
+        return [(n,) for n in names]
+
+    CY = 0.00083
+
+    def V(fn, rd, wr, n, f=1.0):
+        add("V", fn, rd, wr, 0.055 + max(64, n * f) * CY)
+
+    def S(fn, rd, wr, n, f=1.0):
+        add("S", fn, rd, wr, 0.15 + n * f * CY)
+
+    def MM(out, lhsT, rhs, start, stop, rd, wr, n):
+        add("T", lambda g, T: g.tensor.matmul(out(T), lhsT(T), rhs(T), start, stop), rd, wr, max(64, n) * CY * 0.7)
+
+    def tt(o, a, b, op):
+        return lambda g, T: g.vector.tensor_tensor(o(T), a(T), b(T), op)
+
+    def ts(o, a, s1, s2, op0, op1=None):
+        def fn(g, T):
+            x1 = s1(T) if callable_(s1) else s1
+            x2 = s2(T) if callable_(s2) else s2
+            if op1 is None:
+                return g.vector.tensor_scalar(o(T), a(T), x1, x2, op0)
+            return g.vector.tensor_scalar(o(T), a(T), x1, x2, op0, op1)
+        return fn
+
+    def callable_(x):
+        return x is not None and not isinstance(x, (int, float))
+
+    def tc(o, a):
+        return lambda g, T: g.vector.tensor_copy(o(T), a(T))
+
+    def act(o, a, f, **kw):
+        return lambda g, T: g.scalar.activation(o(T), a(T), f, **{k: (v(T) if callable_(v) else v) for k, v in kw.items()})
+
+    def B(name, a=None, b=None, st=None):
+        if a is None:
+            return lambda T: T[name][:]
+        if st is None:
+            return lambda T: T[name][:, a:b]
+        return lambda T: T[name][:, a:b:st]
+
+    def slide(name, k):
+        return lambda T: T[name][:, 15 - k:15 - k + 128]
+
+    nd = [0]
+
+    def load(q, dst, src, cost):
+        k = nd[0]
+        nd[0] += 1
+        add(q, lambda g, T: (g.sync if q == "Y" else g.scalar).dma_start(T[dst][:], T[src][:]), [], al(dst), cost, dma=k)
+
+    load("Y", "SI", "s0", 2.5)
+    load("S", "PI", "p0", 2.5)
+    load("Y", "X", "x0", 6.0)
+    load("S", "PLT", "pl", 6.0)
+    load("Y", "L0", "z0", 6.0)
+    load("Y", "THI", "th", 6.0)
+    load("S", "FA", "f0", 6.0)
+
+    def G(fn, wr, n):
+        add("G", fn, [], wr, 0.15 + 2 * n * CY)
+    G(lambda g, T: g.iota(T.ip[:], [[0, 1]], 0, 1), al("ip"), 1)
+    G(lambda g, T: g.iota(T.irow[:], [[1, 144]], 0, 0), al("irow"), 144)
+    G(lambda g, T: g.iota(T.ibase[:], [[256, 12]], 0, 0), al("ibase"), 12)
+    V(ts(B("ig"), B("ip"), 4, None, A.arith_shift_right), al("ip"), al("ig"), 1)
+    V(tc(B("pf"), B("ip")), al("ip"), al("pf"), 1)
+    V(tc(B("gf"), B("ig")), al("ig"), al("gf"), 1)
+    V(tc(B("row"), B("irow")), al("irow"), al("row"), 144)
+    V(ts(B("igrow"), B("irow", 0, 128), 4, None, A.arith_shift_right), al("irow"), al("igrow"), 128)
+    V(tc(B("grow"), B("igrow")), al("igrow"), al("grow"), 128)
+    V(ts(B("g16"), B("gf"), 16.0, None, A.mult), al("gf"), al("g16"), 1)
+    V(ts(B("g15"), B("gf"), 16.0, 15.0, A.mult, A.add), al("gf"), al("g15"), 1)
+    V(ts(B("p1"), B("pf"), 1.0, None, A.add), al("pf"), al("p1"), 1)
+    V(tt(B("lf"), B("pf"), B("g16"), A.subtract), al("pf", "g16"), al("lf"), 1)
+    V(ts(B("l21"), B("lf"), 2.0, 1.0, A.mult, A.add), al("lf"), al("l21"), 1)
+    V(ts(B("l0"), B("lf"), 0.0, None, A.is_equal), al("lf"), al("l0"), 1)
+    V(ts(B("nl0"), B("l0"), -1.0, None, A.mult), al("l0"), al("nl0"), 1)
+    V(ts(B("nl15"), B("lf"), 15.0, None, A.not_equal), al("lf"), al("nl15"), 1)
+    V(ts(B("r16"), B("lf"), 16.0, 7.5, A.mult, A.add), al("lf"), al("r16"), 1)
+    V(ts(B("base"), B("ibase"), B("r16"), None, A.add), al("ibase", "r16"), al("base"), 12)
+    V(ts(B("W1"), B("row"), B("g15"), None, A.is_equal), al("row", "g15"), al("W1"), 144)
+    V(ts(B("Wm"), B("row"), B("g15"), -1.0, A.is_equal, A.mult), al("row", "g15"), al("Wm"), 144)
+    V(ts(B("W2"), B("row"), B("g15"), 2.0, A.is_equal, A.mult), al("row", "g15"), al("W2"), 144)
+    V(ts(B("Wu"), B("row"), B("g15"), B("l21"), A.is_equal, A.mult), al("row", "g15", "l21"), al("Wu"), 144)
+    V(ts(B("Wh"), B("row"), B("g15"), None, A.is_equal), al("row", "g15"), al("Wh"), 144)
+    R128 = B("row", 0, 128)
+    V(ts(B("Ib"), R128, B("pf"), None, A.is_equal), al("row", "pf"), al("Ib"), 128)
+    V(ts(B("Ihf"), R128, B("pf"), 0.5, A.is_equal, A.mult), al("row", "pf"), al("Ihf"), 128)
+    V(ts(B("I100"), R128, B("pf"), -100.0, A.is_equal, A.mult), al("row", "pf"), al("I100"), 128)
+    V(ts(B("Ih"), R128, B("pf"), None, A.is_equal), al("row", "pf"), al("Ih"), 128)
+    V(ts(B("OB"), B("grow"), B("gf"), None, A.is_equal), al("grow", "gf"), al("OB"), 128)
+    V(ts(B("im8"), B("irow", 0, 128), NC - 1, None, A.bitwise_and), al("irow"), al("im8"), 128)
+    V(ts(B("mk"), B("im8"), NC - NQ - 0.5, -1.0, A.is_lt, A.mult), al("im8"), al("mk"), 128)
+    V(tt(B("OBm"), B("mk"), B("OB"), A.mult), al("mk", "OB"), al("OBm"), 128, 2)
+    V(ts(B("Im"), R128, B("pf"), -1.0, A.is_equal, A.mult), al("row", "pf"), al("Im"), 128)
+    V(ts(B("GT"), R128, B("pf"), None, A.is_gt), al("row", "pf"), al("GT"), 128)
+    V(tt(B("Ls"), B("GT"), B("OB"), A.mult), al("GT", "OB"), al("Ls"), 128, 2)
+    V(tt(B("Li"), B("Ls"), B("Ib"), A.add), al("Ls", "Ib"), al("Li"), 128, 2)
+    V(ts(B("Tp"), R128, B("g16"), None, A.is_equal), al("row", "g16"), al("Tp"), 128)
+    V(tt(B("TpI"), B("Tp"), B("Ih"), A.subtract), al("Tp", "Ih"), al("TpI"), 128, 2)
+    V(ts(B("Sh"), R128, B("p1"), B("nl15"), A.is_equal, A.mult), al("row", "p1", "nl15"), al("Sh"), 128)
+    V(tt(B("ShI"), B("Sh"), B("Ih"), A.subtract), al("Sh", "Ih"), al("ShI"), 128, 2)
+    V(lambda g, T: g.vector.memset(T.cq[:], -0.5), [], al("cq"), I)
+    V(lambda g, T: g.vector.memset(T.c75[:], -7.5), [], al("c75"), 16)
+
+    V(tc(B("PU"), B("PI")), al("PI"), al("PU"), 12)
+    V(tc(B("SU"), B("SI")), al("SI"), al("SU"), I)
+    V(ts(B("E16"), lambda T: T.PLT[:, :].indirect(T.PU[:, 0:12]), -CEN, None, A.add), al("PLT", "PU"), al("E16"), I, 1.6)
+    V(ts(B("EU"), B("E16"), CEN, None, A.add), al("E16"), al("EU"), I)
+    V(ts(B("b5", 0, I), B("SI"), -CEN, None, A.add), al("SI"), [("b5", 0, I)], I)
+    V(tc(B("PF"), B("PI")), al("PI"), al("PF"), 12)
+    V(tc(B("BND"), B("THI")), al("THI"), al("BND"), I)
+
+    def gathers():
+        V(lambda g, T: g.vector.tensor_copy(T.XS[:], T.X[:, :].indirect(T.SU[:, 0:I])), al("X", "SU"), al("XS"), W, 1.5)
+        S(lambda g, T: g.scalar.activation(T.XE[:], T.X[:, :].indirect(T.EU[:, 0:I]), F.Copy), al("X", "EU"), al("XE"), W, 1.5)
+
+    gathers()
+    allqm = [(q, m) for q in range(NC) for m in range(NK)]
+    fast, slow = list(range(NC - NQ)), list(range(NC - NQ, NC))
+    porder = []
+    while fast or slow:
+        if slow and (not fast or len(slow) * (NC - NQ) >= len(fast) * NQ):
+            porder.append(slow.pop(0))
+        else:
+            porder.append(fast.pop(0))
+    for t in range(TURNS):
+        L, Y = "L%d" % t, "Y%d" % t
+        f0, f1 = ("FA", "FB") if t % 2 == 0 else ("FB", "FA")
+        s0, s1 = (0, I) if t % 2 == 0 else (I, 0)
+        if t == 0:
+            for c in range(16):
+                S(act(B("IC", 128 * c, 128 * c + 128), B("Ib"), F.Copy, scale=float(c + 1)), al("Ib"), [("IC", 128 * c, 128 * c + 128)], 128)
+        for k in [k for k in range(16) if k % NC < NC - NQ]:
+            MM(B("b3", 0, I), slide("Wm", k), lambda T, k=k: T.XE[:, k:W:16], k == 0, False, al("Wm", "XE"), [("b3", 0, I)], I)
+        for m in range(NK):
+            MM(B("b0", m, CW, NK), B("Ib"), B(L), True, True, al("Ib", L), [("b0", 0, CW)], I)
+        MM(B("b3", 0, I), B("OBm"), B(L), False, False, al("OBm", L), [("b3", 0, I)], I)
+        for r in range(16):
+            MM(B("b7", 0, 12), slide("Wu", r), B(L, r, I, 16), r == 0, r == 15, al("Wu", L), [("b7", 0, 12)], 12)
+        MM(B("b7", 256, 256 + I), B("Ihf"), B(L), True, False, al("Ihf", L), [("b7", 256, 256 + I)], I)
+        MM(B("b7", 256, 256 + I), B("Ihf"), B(f0), False, False, al("Ihf", f0), [("b7", 256, 256 + I)], I)
+        MM(B("b7", 256, 256 + I), B("Ihf"), B("cq"), False, True, al("Ihf", "cq"), [("b7", 256, 256 + I)], I)
+        V(ts(B(f1), B("b7", 256, 256 + I), MAGIC, MAGIC, A.add, A.subtract), [("b7", 256, 256 + I)], al(f1), I)
+        V(tc(B("H1"), B("b7", 0, 12)), [("b7", 0, 12)], al("H1"), 12)
+        V(ts(B("H2"), B("H1"), 4095, None, A.bitwise_and), al("H1"), al("H2"), 12)
+        V(ts(B("H3"), B("H2"), 1184.0, None, A.add), al("H2"), al("H3"), 12)
+        V(tt(B("H4"), B("H2"), B("H3"), A.mult), al("H2", "H3"), al("H4"), 12)
+        V(ts(B("H7"), B("H4"), 5, PLN - 1, A.arith_shift_right, A.bitwise_and), al("H4"), al("H7"), 12)
+        V(tc(B("PU"), B("H7")), al("H7"), al("PU"), 12)
+        V(ts(B("CAND"), lambda T: T.PLT[:, :].indirect(T.PU[:, 0:12]), -CEN, None, A.add), al("PLT", "PU"), al("CAND"), I, 1.6)
+        V(tt(B("DES"), B("E16"), B("b5", s0, s0 + I), A.subtract), al("E16") + [("b5", s0, s0 + I)], al("DES"), I)
+        for q in range(NC):
+            V(tt(B("D", CW * q, CW * q + CW), lambda T, q=q: T.XS[:, q:W:NC], B("b0", 0, CW), A.subtract),
+              al("XS") + [("b0", 0, CW)], [("D", CW * q, CW * q + CW)], CW)
+        for c in range(4):
+            a, b = 768 * c, 768 * c + 768
+            S(act(B("AB", a, b), B("D", a, b), F.Abs), [("D", a, b)], [("AB", a, b)], 768)
+        for c in range(4):
+            a, b = 768 * c, 768 * c + 768
+            if c < NF:
+                V(ts(B("SG", a, b), B("D", a, b), 0.0, -0.5, A.is_gt, A.add), [("D", a, b)], [("SG", a, b)], 768, 0.5)
+            else:
+                S(act(B("SG", a, b), B("D", a, b), F.Sign, bias=-0.5), [("D", a, b)], [("SG", a, b)], 768)
+        for k, (q, m) in enumerate(allqm):
+            MM(B("b1", 0, I), slide("W1", q + NC * m), B("AB", CW * q + m, CW * q + CW, NK), k == 0, k == 15, al("W1") + [("AB", CW * q, CW * q + CW)], [("b1", 0, I)], I)
+        for k, (q, m) in enumerate(allqm):
+            MM(B("b2", 0, I), slide("W2" if CW * q < 768 * NF else "W1", q + NC * m), B("SG", CW * q + m, CW * q + CW, NK), k == 0, k == 15, al("W1", "W2") + [("SG", CW * q, CW * q + CW)], [("b2", 0, I)], I)
+        for q in range(NC - NQ, NC):
+            bk = "b4" if q % 2 else "b6"
+            for m in range(NK):
+                k = q + NC * m
+                MM(B(bk, I * m, I * m + I), B("Ib"), lambda T, k=k: T.XE[:, k:W:16], True, False, al("Ib", "XE"), [(bk, I * m, I * m + I)], I)
+                MM(B(bk, I * m, I * m + I), B("Im"), B(L), False, True, al("Im", L), [(bk, I * m, I * m + I)], I)
+            S(act(B("MX", CW * q, CW * q + CW), B(bk, 0, CW), F.Abs), [(bk, 0, CW)], [("MX", CW * q, CW * q + CW)], CW)
+        for q in range(NC - NQ):
+            V(tt(B("MX", CW * q, CW * q + CW), lambda T, q=q: T.XE[:, q:W:NC], B("b0", 0, CW), A.max),
+              al("XE") + [("b0", 0, CW)], [("MX", CW * q, CW * q + CW)], CW)
+        pq = [(q, m) for q in porder for m in range(NK)]
+        for (q, m) in pq:
+            k = q + NC * m
+            if q < NC - NQ:
+                MM(B("b3", 0, I), slide("W2", k), B("MX", CW * q + m, CW * q + CW, NK), False, (q, m) == pq[-1], al("W2") + [("MX", CW * q, CW * q + CW)], [("b3", 0, I)], I)
+            else:
+                MM(B("b3", 0, I), slide("W1", k), B("MX", CW * q + I * m, CW * q + I * m + I), False, (q, m) == pq[-1], al("W1") + [("MX", CW * q, CW * q + CW)], [("b3", 0, I)], I)
+        V(tt(B("RS"), B("b1", 0, I), B("BND"), A.is_lt), [("b1", 0, I)] + al("BND"), al("RS"), I)
+        MM(B("b1", I, 2 * I), B("Ls"), B("RS"), True, True, al("Ls", "RS"), [("b1", I, 2 * I)], I)
+        V(tt(B("FI"), B("RS"), B("b1", I, 2 * I), A.is_gt), al("RS") + [("b1", I, 2 * I)], al("FI"), I)
+        V(tt(B("FF"), B("FI"), B("b5", s0, s0 + I), A.mult), al("FI") + [("b5", s0, s0 + I)], al("FF"), I)
+        MM(B("b4", I, 2 * I), B("Li"), B("RS"), True, True, al("Li", "RS"), [("b4", I, 2 * I)], I)
+        S(act(B("b1", 0, I), B("b4", I, 2 * I), F.Relu, scale=-1.0, bias=1.0), [("b4", I, 2 * I)], [("b1", 0, I)], I)
+        S(act(B("KK"), B("b2", 0, I), F.Relu, scale=16.0, bias=128.0), [("b2", 0, I)], al("KK"), I)
+        MM(B("b2", I, 2 * I), B("OB"), B("RS"), True, False, al("OB", "RS"), [("b2", I, 2 * I)], I)
+        MM(B("b2", I, 2 * I), B("I100"), B("FI"), False, True, al("I100", "FI"), [("b2", I, 2 * I)], I)
+        V(tt(B("b2", 0, I), B("b2", I, 2 * I), B("KK"), A.is_gt), [("b2", I, 2 * I)] + al("KK"), [("b2", 0, I)], I)
+        V(tt(B("WD"), B("DES"), B("b2", 0, I), A.mult), al("DES") + [("b2", 0, I)], al("WD"), I)
+        V(tt(B("RR"), B("WD"), B("b5", s0, s0 + I), A.add), al("WD") + [("b5", s0, s0 + I)], al("RR"), I)
+        V(tt(B("QQ"), B("RR"), B("b1", 0, I), A.mult), al("RR") + [("b1", 0, I)], al("QQ"), I)
+        V(tt(B("RP"), B("b3", 0, I), B("BND"), A.is_lt), [("b3", 0, I)] + al("BND"), al("RP"), I)
+        MM(B("b3", I, 2 * I), B("OB"), B("RS"), True, False, al("OB", "RS"), [("b3", I, 2 * I)], I)
+        MM(B("b3", I, 2 * I), B("Ls"), B("RP"), False, True, al("Ls", "RP"), [("b3", I, 2 * I)], I)
+        MM(B("b4", 0, I), B("OB"), B("RS"), True, False, al("OB", "RS"), [("b4", 0, I)], I)
+        MM(B("b4", 0, I), B("OB"), B("RP"), False, True, al("OB", "RP"), [("b4", 0, I)], I)
+        V(tt(B("b6", I, 2 * I), B("RP"), B("b3", I, 2 * I), A.is_gt), al("RP") + [("b3", I, 2 * I)], [("b6", I, 2 * I)], I)
+        S(act(B("b4", I, 2 * I), B("b4", 0, I), F.Relu, scale=B("nl0"), bias=B("l0")), [("b4", 0, I)] + al("nl0", "l0"), [("b4", I, 2 * I)], I)
+        V(tt(B("b6", 0, I), B("E16"), B("b6", I, 2 * I), A.mult), al("E16") + [("b6", I, 2 * I)], [("b6", 0, I)], I)
+        V(tt(B("HH"), B("CAND"), B("b4", I, 2 * I), A.mult), al("CAND") + [("b4", I, 2 * I)], al("HH"), I)
+        V(tt(B("GG"), B("HH"), B("b6", 0, I), A.add), al("HH") + [("b6", 0, I)], al("GG"), I)
+        for src in ("FF", "GG"):
+            for r in range(16):
+                MM(B("b7", 16, 28), slide("Wh", r), B(src, r, I, 16), (src, r) == ("FF", 0), (src, r) == ("GG", 15), al("Wh", src), [("b7", 16, 28)], 12)
+        V(ts(B("TU"), B("b7", 16, 28), CEN, None, A.add), [("b7", 16, 28)], al("TU"), 12)
+        V(lambda g, T, f1=f1: g.vector.tensor_tensor(T.YD[:], T.X[:, :].indirect(T.TU[:, 0:12]), T[f1][:], A.subtract), al("X", "TU", f1), al("YD"), I, 1.6)
+        S(act(B(Y), B("YD"), F.Abs), al("YD"), al(Y), I)
+        if t < TURNS - 1:
+            add("G", ("send", t), al(Y), [], 1.5, send=t)
+            Ln = "L%d" % (t + 1)
+            bl = (-t) % N
+            a, b = BLK * bl, BLK * bl + BLK
+            S(act(B(Ln, a, b), B(Y, a, b), F.Copy), al(Y), [(Ln, a, b)], BLK)
+            wr = [(Ln, c, d) for c, d in ((0, a), (b, I)) if d > c]
+            add("R", None, [], wr, 5.0, arr=t)
+        MM(B("b7", 32, 44), B("Ib"), B("c75", 0, 12), True, False, al("Ib", "c75"), [("b7", 32, 44)], 12)
+        for r in range(16):
+            MM(B("b7", 32, 44), slide("W1", r), B(Y, r, I, 16), False, r == 15, al("W1", Y), [("b7", 32, 44)], 12)
+        MM(B("b0", 0, I), B("Ihf"), B(L), True, False, al("Ihf", L), [("b0", 0, I)], I)
+        MM(B("b0", 0, I), B("Ihf"), B("cq"), False, False, al("Ihf", "cq"), [("b0", 0, I)], I)
+        MM(B("b0", 0, I), B("Ihf"), B(Y), False, True, al("Ihf", Y), [("b0", 0, I)], I)
+        V(ts(B("QF"), B("b7", 32, 44), MAGIC16, MAGIC16, A.add, A.subtract), [("b7", 32, 44)], al("QF"), 12)
+        V(tt(B("RF"), B("base"), B("b7", 32, 44), A.add), al("base") + [("b7", 32, 44)], al("RF"), 12)
+        V(tt(B("MF"), B("RF"), B("QF"), A.subtract), al("RF", "QF"), al("MF"), 12)
+        V(tc(B("MU"), B("MF")), al("MF"), al("MU"), 12)
+        V(ts(B("WR"), B("b0", 0, I), MAGIC, MAGIC, A.add, A.subtract), [("b0", 0, I)], al("WR"), I)
+        V(lambda g, T: g.vector.tensor_copy(T.X[:, :].indirect(T.MU[:, 0:12]), T.WR[:]), al("WR", "MU", "X"), al("X"), I, 3.5)
+        o = (B("b5", s1, s1 + I), [("b5", s1, s1 + I)])
+        MM(o[0], B("Ih"), B("RR"), True, False, al("Ih", "RR"), o[1], I)
+        MM(o[0], B("ShI"), B("QQ"), False, False, al("ShI", "QQ"), o[1], I)
+        MM(o[0], B("TpI"), B("FF"), False, False, al("TpI", "FF"), o[1], I)
+        MM(o[0], B("Tp"), B("GG"), False, True, al("Tp", "GG"), o[1], I)
+        last = t == TURNS - 1
+        if last:
+            V(ts(B("OS"), o[0], CEN, None, A.add), o[1], al("OS"), I)
+        else:
+            V(ts(B("SU"), o[0], CEN, None, A.add), o[1], al("SU"), I)
+        S(act(B("CR"), B("b4", 0, I), F.Relu, scale=B("nl0"), bias=B("l0")), [("b4", 0, I)] + al("nl0", "l0"), al("CR"), I)
+        S(act(B("C64"), B("b4", 0, I), F.Relu, scale=-64.0, bias=64.0), [("b4", 0, I)], al("C64"), I)
+        if not last:
+            S(act(B("b3", 0, I), B("b4", 0, I), F.Relu, scale=-1.0, bias=1.0), [("b4", 0, I)], [("b3", 0, I)], I)
+            S(act(B("b3", I, 2 * I), B("b4", 0, I), F.Sign), [("b4", 0, I)], [("b3", I, 2 * I)], I)
+            V(tt(B("b6", 0, I), B("E16"), B("b3", I, 2 * I), A.mult), al("E16") + [("b3", I, 2 * I)], [("b6", 0, I)], I)
+            V(tt(B("HF"), B("CAND"), B("b3", 0, I), A.mult), al("CAND") + [("b3", 0, I)], al("HF"), I)
+            V(tt(B("E16"), B("HF"), B("b6", 0, I), A.add), al("HF") + [("b6", 0, I)], al("E16"), I)
+            V(ts(B("EU"), B("E16"), CEN, None, A.add), al("E16"), al("EU"), I, 0.5)
+        V(tt(B("BND"), B("BND"), B("C64"), A.add), al("BND", "C64"), al("BND"), I, 2)
+        if not last:
+            gathers()
+        for r in range(16):
+            MM(B("b2", 384, 396), slide("W1", r), B("CR", r, I, 16), r == 0, r == 15, al("W1", "CR"), [("b2", 384, 396)], 12)
+        V(tt(B("DP"), B("H7"), B("PF"), A.subtract), al("H7", "PF"), al("DP"), 12)
+        V(tt(B("DQ"), B("DP"), B("b2", 384, 396), A.mult), al("DP") + [("b2", 384, 396)], al("DQ"), 12)
+        V(tt(B("PF"), B("PF"), B("DQ"), A.add), al("PF", "DQ"), al("PF"), 12)
+        if last:
+            V(tt(B("CR"), B("BND"), B("THI"), A.subtract), al("BND", "THI"), al("CR"), I, 2)
+            for r in range(16):
+                MM(B("b2", 384, 396), slide("W1", r), B("CR", r, I, 16), r == 0, r == 15, al("W1", "CR"), [("b2", 384, 396)], 12)
+            def store(dst, src):
+                k = nd[0]
+                nd[0] += 1
+                add("Y", lambda g, T: g.sync.dma_start(T[dst][:], T[src][:]), al(src), [], 2.5, dma=k)
+            store("yf", f1)
+            store("ys", "OS")
+            V(ts(B("MF"), B("b2", 384, 396), PLN / 1024.0, None, A.mult), [("b2", 384, 396)], al("MF"), 12)
+            V(tt(B("YPF"), B("MF"), B("PF"), A.add), al("MF", "PF"), al("YPF"), 12)
+            store("yp", "YPF")
+            for c in range(16):
+                MM(B("b0", 0, I), B("IC", 128 * c, 128 * c + 128), B("X", c, W, 16), c == 0, c == 15, [("IC", 128 * c, 128 * c + 128), ("X",)], [("b0", 0, I)], I)
+            S(act(B("OX"), B("b0", 0, I), F.Copy), [("b0", 0, I)], al("OX"), I)
+            store("yx", "OX")
+    return ops
+
+
+def _deps(ops):
+    data, order = [], []
+    acc = {}
+    banks = {}
+    sends = {}
+    for i, (q, fn, rd, wr, cost, kw) in enumerate(ops):
+        dd, oo = set(), set()
+        seen = {}
+        for lst, w in ((rd, False), (wr, True)):
+            for (n, a, b) in lst:
+                if n[0] == "b" and n[1:].isdigit():
+                    e = seen.get(n)
+                    if e is None:
+                        e = banks.setdefault(n, {"q": q, "cur": [], "prev": []})
+                        if e["q"] != q:
+                            e["prev"], e["cur"], e["q"] = [x[0] for x in e["cur"]], [], q
+                        seen[n] = e
+                        dd.update(e["prev"])
+                    if q == "T":
+                        if e["cur"] and e["cur"][-1][0] != i:
+                            oo.add(e["cur"][-1][0])
+                    else:
+                        for (j, c, d, w2) in e["cur"]:
+                            if j != i and (w or w2) and c < b and a < d:
+                                dd.add(j)
+                    e["cur"].append((i, a, b, w))
+                else:
+                    l = acc.setdefault(n, [])
+                    for (j, c, d, w2) in l:
+                        if j != i and (w or w2) and c < b and a < d:
+                            dd.add(j)
+        for lst, w in ((rd, False), (wr, True)):
+            for (n, a, b) in lst:
+                if n[0] == "b" and n[1:].isdigit():
+                    continue
+                l = acc[n]
+                if w:
+                    l[:] = [x for x in l if not (a <= x[1] and x[2] <= b and x[0] != i)]
+                l.append((i, a, b, w))
+        if "send" in kw:
+            sends[kw["send"]] = i
+        if "arr" in kw:
+            oo.add(sends[kw["arr"]])
+        dd.discard(i)
+        oo -= dd
+        data.append(sorted(dd))
+        order.append(sorted(oo))
+    return data, order
+
+
+def _schedule(ops, data, order):
+    n = len(ops)
+    succ = [[] for _ in range(n)]
+    for i in range(n):
+        for j in data[i] + order[i]:
+            succ[j].append(i)
+    prio = [0.0] * n
+    for i in range(n - 1, -1, -1):
+        prio[i] = ops[i][4] + max([prio[k] + LAT for k in succ[i]], default=0.0)
+    base = list(prio)
+    for i in range(n):
+        if ops[i][3]:
+            w = ops[i][3][0]
+            prio[i] = base[i] + BONUS.get("%s:%s:%d" % (ops[i][0], w[0], w[1]), 0.0)
+    left = [len(data[i]) + len(order[i]) for i in range(n)]
+    ready = [0.0] * n
+    pool = {}
+    free = {}
+    for i in range(n):
+        if left[i] == 0:
+            pool.setdefault(ops[i][0], []).append(i)
+    out = []
+    while True:
+        best = None
+        for q, l in pool.items():
+            if not l:
+                continue
+            st = max(free.get(q, 0.0), min(ready[i] for i in l))
+            if best is None or st < best[0]:
+                best = (st, q)
+        if best is None:
+            break
+        st, q = best
+        i = max((i for i in pool[q] if ready[i] <= st + 1e-9), key=lambda i: (prio[i], -i))
+        pool[q].remove(i)
+        dma = "dma" in ops[i][5] or q == "R"
+        fin = st + ops[i][4]
+        free[q] = st + (0.1 if dma else ops[i][4])
+        out.append((i, st, fin))
+        for k in succ[i]:
+            same = ops[k][0] == q and i in order[k]
+            ready[k] = max(ready[k], fin if same else fin + LAT)
+            left[k] -= 1
+            if left[k] == 0:
+                pool.setdefault(ops[k][0], []).append(k)
+    return out
+
+
+_PLAN = {}
+
+
+def _plan():
+    if not _PLAN:
+        ops = _build()
+        data, order = _deps(ops)
+        _PLAN["ops"], _PLAN["data"], _PLAN["sched"] = ops, data, _schedule(ops, data, order)
+    return _PLAN["ops"], _PLAN["data"], _PLAN["sched"]
+
+
+def rank_program(g, core, T, topo):
+    rank = T.rank_of(core)
+    if rank is None:
+        return
+    ops, data, sched = _plan()
+    eng = {"V": g.vector, "S": g.scalar, "T": g.tensor, "G": g, "Y": g.sync}
+    seq, cnt, clock = {}, {}, {}
+    know = {q: {} for q in eng}
+
+    def send(t):
+        tr = []
+        used = 0
+        for b in range(N):
+            to = (rank + b + t) % N
+            if to == rank:
+                continue
+            dst = T.cores[to]
+            rid, pnc = topo.addr(dst)[:2]
+            e = topo.engines(core, dst)
+            tr.append(RemoteDMATransfer(dst_ids=[DstId(rid=rid, pnc=pnc)], dma_engine_mask=1 << e[used % len(e)], remote_sem=T.sem["arr%d" % t],
+                                        src=T["Y%d" % t][:, BLK * b:BLK * b + BLK], dst=T["L%d" % (t + 1)][:, BLK * b:BLK * b + BLK]))
+            used += 1
+        g.remote_dma_fused(tr, local_sem=T.sem.sent)
+        return used
+
+    sent = 0
+    dmas = []
+    for (i, st, fin) in sched:
+        q, fn, rd, wr, cost, kw = ops[i]
+        if q == "R":
+            seq[i] = ("arr%d" % kw["arr"], N - 1)
+            clock[i] = {}
+            continue
+        kn = know[q]
+        need = {}
+        for j in data[i]:
+            s, v = seq[j]
+            if kn.get(s, 0) < v:
+                need[s] = max(need.get(s, 0), v)
+        for j in sorted(data[i], key=lambda j: -j):
+            s, v = seq[j]
+            if s in need and need[s] == v:
+                for s2, v2 in clock[j].items():
+                    if s2 in need and s2 != s and need[s2] <= v2:
+                        del need[s2]
+        for j in data[i]:
+            s, v = seq[j]
+            for s2, v2 in list(clock[j].items()) + [(s, v)]:
+                if kn.get(s2, 0) < v2:
+                    kn[s2] = v2
+        for s, v in need.items():
+            eng[q].wait_ge(T.sem[s], v)
+        if "send" in kw:
+            sent += send(kw["send"])
+            continue
+        ins = fn(g, T)
+        if "dma" in kw:
+            s = "dm%d" % kw["dma"]
+            ins.then_inc(T.sem[s], 16)
+            seq[i] = (s, 16)
+            dmas.append(s)
+            clock[i] = dict(kn)
+        else:
+            s = "q" + q
+            cnt[s] = cnt.get(s, 0) + 1
+            ins.then_inc(T.sem[s], 1)
+            seq[i] = (s, cnt[s])
+            clock[i] = dict(kn)
+    g.wait_ge(T.sem.sent, sent)
+    for s, v in cnt.items():
+        g.wait_ge(T.sem[s], v)
+    for s in dmas:
+        g.wait_ge(T.sem[s], 16)

@@ -6,8 +6,12 @@ A = AluOpType
 F = ActivationFunctionType
 I, W, PLN, TURNS, BLK, N = 192, 3072, 2048, 8, 24, 8
 NK = 2
-NQ = 1
+NQ = 0
 NF = 0
+NS = 2
+CSPL = 152
+XC = 3
+TR = 0.5
 NC = 16 // NK
 CW = NK * I
 CEN = 1536.0
@@ -51,7 +55,7 @@ SCRATCH = {
     "Ls": ("sbuf", [128, 128], "bfloat16"), "Li": ("sbuf", [128, 128], "bfloat16"),
     "Ih": ("sbuf", [128, 128], "float16"), "Sh": ("sbuf", [128, 128], "float16"),
     "ShI": ("sbuf", [128, 128], "float16"), "Tp": ("sbuf", [128, 128], "float16"), "TpI": ("sbuf", [128, 128], "float16"),
-    "cq": ("sbuf", [128, I], "bfloat16"), "c75": ("sbuf", [128, 16], "bfloat16"),
+    "cq": ("sbuf", [128, I], "bfloat16"), "zz": ("sbuf", [128, I], "bfloat16"), "c75": ("sbuf", [128, 16], "bfloat16"),
     "IC": ("sbuf", [128, 16 * 128], "bfloat16"),
     "OS": ("sbuf", [128, I], "float32"), "OX": ("sbuf", [128, I], "float32"),
 }
@@ -64,6 +68,7 @@ NDMA = 12
 SEMAPHORES = ["qV", "qS", "qT", "qG", "sent"] + ["arr%d" % t for t in range(8)] + ["dm%d" % k for k in range(NDMA)]
 
 LAT = 0.08
+HOLD = 0.15
 BONUS = {}
 
 
@@ -85,7 +90,7 @@ def _build():
         add("S", fn, rd, wr, 0.15 + n * f * CY)
 
     def MM(out, lhsT, rhs, start, stop, rd, wr, n):
-        add("T", lambda g, T: g.tensor.matmul(out(T), lhsT(T), rhs(T), start, stop), rd, wr, max(64, n) * CY * 0.7)
+        add("T", lambda g, T: g.tensor.matmul(out(T), lhsT(T), rhs(T), start, stop), rd, wr, max(64, n) * CY * TR)
 
     def tt(o, a, b, op):
         return lambda g, T: g.vector.tensor_tensor(o(T), a(T), b(T), op)
@@ -176,6 +181,7 @@ def _build():
     V(tt(B("TpI"), B("Tp"), B("Ih"), A.subtract), al("Tp", "Ih"), al("TpI"), 128, 2)
     V(ts(B("Sh"), R128, B("p1"), B("nl15"), A.is_equal, A.mult), al("row", "p1", "nl15"), al("Sh"), 128)
     V(tt(B("ShI"), B("Sh"), B("Ih"), A.subtract), al("Sh", "Ih"), al("ShI"), 128, 2)
+    V(lambda g, T: g.vector.memset(T.zz[:], 0.0), [], al("zz"), I)
     V(lambda g, T: g.vector.memset(T.cq[:], -0.5), [], al("cq"), I)
     V(lambda g, T: g.vector.memset(T.c75[:], -7.5), [], al("c75"), 16)
 
@@ -188,18 +194,32 @@ def _build():
     V(tc(B("BND"), B("THI")), al("THI"), al("BND"), I)
 
     def gathers():
-        V(lambda g, T: g.vector.tensor_copy(T.XS[:], T.X[:, :].indirect(T.SU[:, 0:I])), al("X", "SU"), al("XS"), W, 1.5)
-        S(lambda g, T: g.scalar.activation(T.XE[:], T.X[:, :].indirect(T.EU[:, 0:I]), F.Copy), al("X", "EU"), al("XE"), W, 1.5)
+        cs = CSPL
+        V(lambda g, T: g.vector.tensor_copy(T.XS[:, 0:16 * cs], T.X[:, :].indirect(T.SU[:, 0:cs])), al("X", "SU"), [("XS", 0, 16 * cs)], 16 * cs, 1.5)
+        if cs < I:
+            S(lambda g, T: g.scalar.activation(T.XS[:, 16 * cs:W], T.X[:, :].indirect(T.SU[:, cs:I]), F.Copy), al("X", "SU"), [("XS", 16 * cs, W)], 16 * (I - cs), 1.5)
+        for c in range(XC):
+            a, b = I // XC * c, I // XC * (c + 1)
+            S(lambda g, T, a=a, b=b: g.scalar.activation(T.XE[:, 16 * a:16 * b], T.X[:, :].indirect(T.EU[:, a:b]), F.Copy), al("X", "EU"), [("XE", 16 * a, 16 * b)], 16 * (b - a), 1.5)
 
     gathers()
-    allqm = [(q, m) for q in range(NC) for m in range(NK)]
-    fast, slow = list(range(NC - NQ)), list(range(NC - NQ, NC))
-    porder = []
-    while fast or slow:
-        if slow and (not fast or len(slow) * (NC - NQ) >= len(fast) * NQ):
-            porder.append(slow.pop(0))
-        else:
-            porder.append(fast.pop(0))
+
+    def mixed(n):
+        fast, slow = list(range(NC - n)), list(range(NC - n, NC))
+        res = []
+        while fast or slow:
+            if slow and (not fast or len(slow) * (NC - n) >= len(fast) * n):
+                res.append(slow.pop(0))
+            else:
+                res.append(fast.pop(0))
+        return res
+
+    turn_bank = [0]
+
+    def bank():
+        turn_bank[0] += 1
+        return "b4" if turn_bank[0] % 2 else "b6"
+
     for t in range(TURNS):
         L, Y = "L%d" % t, "Y%d" % t
         f0, f1 = ("FA", "FB") if t % 2 == 0 else ("FB", "FA")
@@ -207,8 +227,11 @@ def _build():
         if t == 0:
             for c in range(16):
                 S(act(B("IC", 128 * c, 128 * c + 128), B("Ib"), F.Copy, scale=float(c + 1)), al("Ib"), [("IC", 128 * c, 128 * c + 128)], 128)
-        for k in [k for k in range(16) if k % NC < NC - NQ]:
-            MM(B("b3", 0, I), slide("Wm", k), lambda T, k=k: T.XE[:, k:W:16], k == 0, False, al("Wm", "XE"), [("b3", 0, I)], I)
+        MM(B("b3", 0, I), B("Ib"), B("zz"), True, False, al("Ib", "zz"), [("b3", 0, I)], I)
+        for c in range(XC):
+            p, q = I // XC * c, I // XC * (c + 1)
+            for k in [k for k in range(16) if k % NC < NC - NQ]:
+                MM(B("b3", p, q), slide("Wm", k), B("XE", 16 * p + k, 16 * q, 16), False, False, al("Wm") + [("XE", 16 * p, 16 * q)], [("b3", p, q)], q - p)
         for m in range(NK):
             MM(B("b0", m, CW, NK), B("Ib"), B(L), True, True, al("Ib", L), [("b0", 0, CW)], I)
         MM(B("b3", 0, I), B("OBm"), B(L), False, False, al("OBm", L), [("b3", 0, I)], I)
@@ -226,33 +249,50 @@ def _build():
         V(tc(B("PU"), B("H7")), al("H7"), al("PU"), 12)
         V(ts(B("CAND"), lambda T: T.PLT[:, :].indirect(T.PU[:, 0:12]), -CEN, None, A.add), al("PLT", "PU"), al("CAND"), I, 1.6)
         V(tt(B("DES"), B("E16"), B("b5", s0, s0 + I), A.subtract), al("E16") + [("b5", s0, s0 + I)], al("DES"), I)
-        for q in range(NC):
-            V(tt(B("D", CW * q, CW * q + CW), lambda T, q=q: T.XS[:, q:W:NC], B("b0", 0, CW), A.subtract),
-              al("XS") + [("b0", 0, CW)], [("D", CW * q, CW * q + CW)], CW)
-        for c in range(4):
-            a, b = 768 * c, 768 * c + 768
-            S(act(B("AB", a, b), B("D", a, b), F.Abs), [("D", a, b)], [("AB", a, b)], 768)
-        for c in range(4):
-            a, b = 768 * c, 768 * c + 768
-            if c < NF:
-                V(ts(B("SG", a, b), B("D", a, b), 0.0, -0.5, A.is_gt, A.add), [("D", a, b)], [("SG", a, b)], 768, 0.5)
-            else:
-                S(act(B("SG", a, b), B("D", a, b), F.Sign, bias=-0.5), [("D", a, b)], [("SG", a, b)], 768)
-        for k, (q, m) in enumerate(allqm):
-            MM(B("b1", 0, I), slide("W1", q + NC * m), B("AB", CW * q + m, CW * q + CW, NK), k == 0, k == 15, al("W1") + [("AB", CW * q, CW * q + CW)], [("b1", 0, I)], I)
-        for k, (q, m) in enumerate(allqm):
-            MM(B("b2", 0, I), slide("W2" if CW * q < 768 * NF else "W1", q + NC * m), B("SG", CW * q + m, CW * q + CW, NK), k == 0, k == 15, al("W1", "W2") + [("SG", CW * q, CW * q + CW)], [("b2", 0, I)], I)
-        for q in range(NC - NQ, NC):
-            bk = "b4" if q % 2 else "b6"
+        def tensor_diff(X, q, bk):
             for m in range(NK):
                 k = q + NC * m
-                MM(B(bk, I * m, I * m + I), B("Ib"), lambda T, k=k: T.XE[:, k:W:16], True, False, al("Ib", "XE"), [(bk, I * m, I * m + I)], I)
+                MM(B(bk, I * m, I * m + I), B("Ib"), lambda T, k=k: T[X][:, k:W:16], True, False, al("Ib", X), [(bk, I * m, I * m + I)], I)
                 MM(B(bk, I * m, I * m + I), B("Im"), B(L), False, True, al("Im", L), [(bk, I * m, I * m + I)], I)
+
+        VQ = NC - NS
+        for q in range(VQ):
+            V(tt(B("D", CW * q, CW * q + CW), lambda T, q=q: T.XS[:, q:W:NC], B("b0", 0, CW), A.subtract),
+              al("XS") + [("b0", 0, CW)], [("D", CW * q, CW * q + CW)], CW)
+        chunks = [(c, min(VQ, c + 2)) for c in range(0, VQ, 2)]
+        for c, e in chunks:
+            a, b = CW * c, CW * e
+            S(act(B("AB", a, b), B("D", a, b), F.Abs), [("D", a, b)], [("AB", a, b)], b - a)
+        for q in range(VQ, NC):
+            bk = bank()
+            tensor_diff("XS", q, bk)
+            S(act(B("AB", CW * q, CW * q + CW), B(bk, 0, CW), F.Abs), [(bk, 0, CW)], [("AB", CW * q, CW * q + CW)], CW)
+            S(act(B("SG", CW * q, CW * q + CW), B(bk, 0, CW), F.Sign, bias=-0.5), [(bk, 0, CW)], [("SG", CW * q, CW * q + CW)], CW)
+        for c, e in chunks:
+            a, b = CW * c, CW * e
+            if c < 2 * NF:
+                V(ts(B("SG", a, b), B("D", a, b), 0.0, -0.5, A.is_gt, A.add), [("D", a, b)], [("SG", a, b)], b - a, 0.5)
+            else:
+                S(act(B("SG", a, b), B("D", a, b), F.Sign, bias=-0.5), [("D", a, b)], [("SG", a, b)], b - a)
+
+        def piece(buf, q, m, direct):
+            return B(buf, CW * q + I * m, CW * q + I * m + I) if direct else B(buf, CW * q + m, CW * q + CW, NK)
+
+        sq = [(q, m) for q in mixed(NS) for m in range(NK)]
+        for (q, m) in sq:
+            MM(B("b1", 0, I), slide("W1", q + NC * m), piece("AB", q, m, q >= VQ), (q, m) == sq[0], (q, m) == sq[-1], al("W1") + [("AB", CW * q, CW * q + CW)], [("b1", 0, I)], I)
+        gq = sq if NS == 0 else [x for x in sq if x[0] >= VQ] + [x for x in sq if x[0] < VQ]
+        for (q, m) in gq:
+            w = "W2" if q < min(VQ, 2 * NF) else "W1"
+            MM(B("b2", 0, I), slide(w, q + NC * m), piece("SG", q, m, q >= VQ), (q, m) == gq[0], (q, m) == gq[-1], al(w) + [("SG", CW * q, CW * q + CW)], [("b2", 0, I)], I)
+        for q in range(NC - NQ, NC):
+            bk = bank()
+            tensor_diff("XE", q, bk)
             S(act(B("MX", CW * q, CW * q + CW), B(bk, 0, CW), F.Abs), [(bk, 0, CW)], [("MX", CW * q, CW * q + CW)], CW)
         for q in range(NC - NQ):
             V(tt(B("MX", CW * q, CW * q + CW), lambda T, q=q: T.XE[:, q:W:NC], B("b0", 0, CW), A.max),
               al("XE") + [("b0", 0, CW)], [("MX", CW * q, CW * q + CW)], CW)
-        pq = [(q, m) for q in porder for m in range(NK)]
+        pq = [(q, m) for q in mixed(NQ) for m in range(NK)]
         for (q, m) in pq:
             k = q + NC * m
             if q < NC - NQ:
@@ -289,13 +329,13 @@ def _build():
         V(lambda g, T, f1=f1: g.vector.tensor_tensor(T.YD[:], T.X[:, :].indirect(T.TU[:, 0:12]), T[f1][:], A.subtract), al("X", "TU", f1), al("YD"), I, 1.6)
         S(act(B(Y), B("YD"), F.Abs), al("YD"), al(Y), I)
         if t < TURNS - 1:
-            add("G", ("send", t), al(Y), [], 1.5, send=t)
+            add("G", ("send", t), al(Y), [], 1.2, send=t)
             Ln = "L%d" % (t + 1)
             bl = (-t) % N
             a, b = BLK * bl, BLK * bl + BLK
             S(act(B(Ln, a, b), B(Y, a, b), F.Copy), al(Y), [(Ln, a, b)], BLK)
             wr = [(Ln, c, d) for c, d in ((0, a), (b, I)) if d > c]
-            add("R", None, [], wr, 5.0, arr=t)
+            add("R", None, [], wr, 3.8, arr=t)
         MM(B("b7", 32, 44), B("Ib"), B("c75", 0, 12), True, False, al("Ib", "c75"), [("b7", 32, 44)], 12)
         for r in range(16):
             MM(B("b7", 32, 44), slide("W1", r), B(Y, r, I, 16), False, r == 15, al("W1", Y), [("b7", 32, 44)], 12)
@@ -439,6 +479,9 @@ def _schedule(ops, data, order):
             break
         st, q = best
         i = max((i for i in pool[q] if ready[i] <= st + 1e-9), key=lambda i: (prio[i], -i))
+        if ops[i][4] > 0.3:
+            i = max((k for k in pool[q] if ready[k] <= st + HOLD), key=lambda i: (prio[i], -i))
+            st = max(st, ready[i])
         pool[q].remove(i)
         dma = "dma" in ops[i][5] or q == "R"
         fin = st + ops[i][4]
@@ -499,17 +542,18 @@ def rank_program(g, core, T, topo):
             continue
         kn = know[q]
         need = {}
-        for j in data[i]:
+        before = [j for j in data[i] if "send" not in ops[j][5]]
+        for j in before:
             s, v = seq[j]
             if kn.get(s, 0) < v:
                 need[s] = max(need.get(s, 0), v)
-        for j in sorted(data[i], key=lambda j: -j):
+        for j in sorted(before, key=lambda j: -j):
             s, v = seq[j]
             if s in need and need[s] == v:
                 for s2, v2 in clock[j].items():
                     if s2 in need and s2 != s and need[s2] <= v2:
                         del need[s2]
-        for j in data[i]:
+        for j in before:
             s, v = seq[j]
             for s2, v2 in list(clock[j].items()) + [(s, v)]:
                 if kn.get(s2, 0) < v2:

import numpy as np
from concourse.bass import DstId, RemoteDMATransfer
from concourse.mybir import dt, AluOpType, AxisListType, ActivationFunctionType

A = AluOpType
F = ActivationFunctionType
I, W, PLN, TURNS, BLK, N = 192, 3072, 2048, 8, 24, 8
NK = 2
NQ = 0
NF = 0
NS = 2
CSPL = 152
XC = 3
TR = 0.5
NC = 16 // NK
CW = NK * I
CEN = 1536.0
MAGIC = 12582912.0
MAGIC16 = 201326592.0

SCRATCH = {
    "X": ("sbuf", [128, W], "bfloat16"),
    "XS": ("sbuf", [128, W], "bfloat16"), "XE": ("sbuf", [128, W], "bfloat16"),
    "D": ("sbuf", [128, W], "bfloat16"), "AB": ("sbuf", [128, W], "bfloat16"),
    "SG": ("sbuf", [128, W], "bfloat16"), "MX": ("sbuf", [128, W], "bfloat16"),
    "PLT": ("sbuf", [128, PLN], "int32"), "SI": ("sbuf", [128, I], "int32"), "THI": ("sbuf", [128, I], "int32"),
    "PI": ("sbuf", [128, 12], "int32"), "PF": ("sbuf", [128, 12], "float32"),
    "BND": ("sbuf", [128, I], "float32"), "C64": ("sbuf", [128, I], "float32"), "KK": ("sbuf", [128, I], "float32"),
    "RS": ("sbuf", [128, I], "bfloat16"), "RP": ("sbuf", [128, I], "bfloat16"), "FI": ("sbuf", [128, I], "bfloat16"),
    "CR": ("sbuf", [128, I], "bfloat16"), "DES": ("sbuf", [128, I], "float32"), "WD": ("sbuf", [128, I], "float32"),
    "RR": ("sbuf", [128, I], "float16"), "QQ": ("sbuf", [128, I], "float16"), "FF": ("sbuf", [128, I], "float16"),
    "GG": ("sbuf", [128, I], "float16"), "HH": ("sbuf", [128, I], "float16"), "HF": ("sbuf", [128, I], "float16"),
    "E16": ("sbuf", [128, I], "float16"), "CAND": ("sbuf", [128, I], "float16"),
    "SU": ("sbuf", [128, I], "uint16"), "EU": ("sbuf", [128, I], "uint16"),
    "TU": ("sbuf", [128, 12], "uint16"), "PU": ("sbuf", [128, 12], "uint16"), "MU": ("sbuf", [128, 12], "uint16"),
    "FA": ("sbuf", [128, I], "bfloat16"), "FB": ("sbuf", [128, I], "bfloat16"),
    "YD": ("sbuf", [128, I], "bfloat16"), "WR": ("sbuf", [128, I], "bfloat16"),
    "H1": ("sbuf", [128, 12], "int32"), "H2": ("sbuf", [128, 12], "int32"), "H3": ("sbuf", [128, 12], "int32"),
    "H4": ("sbuf", [128, 12], "int32"),
    "H7": ("sbuf", [128, 12], "int32"), "DP": ("sbuf", [128, 12], "float32"), "DQ": ("sbuf", [128, 12], "float32"),
    "QF": ("sbuf", [128, 12], "float32"), "RF": ("sbuf", [128, 12], "float32"), "MF": ("sbuf", [128, 12], "float32"),
    "YPF": ("sbuf", [128, 12], "float32"),
    "ip": ("sbuf", [128, 1], "int32"), "ig": ("sbuf", [128, 1], "int32"), "irow": ("sbuf", [128, 144], "int32"),
    "igrow": ("sbuf", [128, 128], "int32"), "ibase": ("sbuf", [128, 12], "int32"),
    "pf": ("sbuf", [128, 1], "float32"), "p1": ("sbuf", [128, 1], "float32"), "gf": ("sbuf", [128, 1], "float32"),
    "g16": ("sbuf", [128, 1], "float32"), "g15": ("sbuf", [128, 1], "float32"), "lf": ("sbuf", [128, 1], "float32"),
    "l21": ("sbuf", [128, 1], "float32"), "l0": ("sbuf", [128, 1], "float32"), "nl0": ("sbuf", [128, 1], "float32"),
    "nl15": ("sbuf", [128, 1], "float32"), "r16": ("sbuf", [128, 1], "float32"),
    "row": ("sbuf", [128, 144], "float32"), "grow": ("sbuf", [128, 128], "float32"), "base": ("sbuf", [128, 12], "float32"),
    "W1": ("sbuf", [128, 144], "bfloat16"), "W2": ("sbuf", [128, 144], "bfloat16"), "Wm": ("sbuf", [128, 144], "bfloat16"),
    "Wu": ("sbuf", [128, 144], "bfloat16"), "Wh": ("sbuf", [128, 144], "float16"),
    "OB": ("sbuf", [128, 128], "bfloat16"), "OBm": ("sbuf", [128, 128], "bfloat16"), "Ib": ("sbuf", [128, 128], "bfloat16"),
    "Im": ("sbuf", [128, 128], "bfloat16"), "im8": ("sbuf", [128, 128], "int32"), "mk": ("sbuf", [128, 128], "float32"),
    "Ihf": ("sbuf", [128, 128], "bfloat16"), "I100": ("sbuf", [128, 128], "bfloat16"), "GT": ("sbuf", [128, 128], "bfloat16"),
    "Ls": ("sbuf", [128, 128], "bfloat16"), "Li": ("sbuf", [128, 128], "bfloat16"),
    "Ih": ("sbuf", [128, 128], "float16"), "Sh": ("sbuf", [128, 128], "float16"),
    "ShI": ("sbuf", [128, 128], "float16"), "Tp": ("sbuf", [128, 128], "float16"), "TpI": ("sbuf", [128, 128], "float16"),
    "cq": ("sbuf", [128, I], "bfloat16"), "zz": ("sbuf", [128, I], "bfloat16"), "c75": ("sbuf", [128, 16], "bfloat16"),
    "IC": ("sbuf", [128, 16 * 128], "bfloat16"),
    "OS": ("sbuf", [128, I], "float32"), "OX": ("sbuf", [128, I], "float32"),
}
for _t in range(8):
    SCRATCH["L%d" % _t] = ("sbuf", [128, I], "bfloat16")
    SCRATCH["Y%d" % _t] = ("sbuf", [128, I], "bfloat16")
for _t in range(8):
    SCRATCH["b%d" % _t] = ("psum", [128, 512], "float32")
NDMA = 12
SEMAPHORES = ["qV", "qS", "qT", "qG", "sent"] + ["arr%d" % t for t in range(8)] + ["dm%d" % k for k in range(NDMA)]

LAT = 0.08
HOLD = 0.15
BONUS = {}


def _build():
    ops = []

    def add(q, fn, rd, wr, cost, **kw):
        ops.append([q, fn, [(r if len(r) == 3 else (r[0], 0, 1 << 20)) for r in rd], [(r if len(r) == 3 else (r[0], 0, 1 << 20)) for r in wr], cost, kw])

    def al(*names):
        return [(n,) for n in names]

    CY = 0.00083

    def V(fn, rd, wr, n, f=1.0):
        add("V", fn, rd, wr, 0.055 + max(64, n * f) * CY)

    def S(fn, rd, wr, n, f=1.0):
        add("S", fn, rd, wr, 0.15 + n * f * CY)

    def MM(out, lhsT, rhs, start, stop, rd, wr, n):
        add("T", lambda g, T: g.tensor.matmul(out(T), lhsT(T), rhs(T), start, stop), rd, wr, max(64, n) * CY * TR)

    def tt(o, a, b, op):
        return lambda g, T: g.vector.tensor_tensor(o(T), a(T), b(T), op)

    def ts(o, a, s1, s2, op0, op1=None):
        def fn(g, T):
            x1 = s1(T) if callable_(s1) else s1
            x2 = s2(T) if callable_(s2) else s2
            if op1 is None:
                return g.vector.tensor_scalar(o(T), a(T), x1, x2, op0)
            return g.vector.tensor_scalar(o(T), a(T), x1, x2, op0, op1)
        return fn

    def callable_(x):
        return x is not None and not isinstance(x, (int, float))

    def tc(o, a):
        return lambda g, T: g.vector.tensor_copy(o(T), a(T))

    def act(o, a, f, **kw):
        return lambda g, T: g.scalar.activation(o(T), a(T), f, **{k: (v(T) if callable_(v) else v) for k, v in kw.items()})

    def B(name, a=None, b=None, st=None):
        if a is None:
            return lambda T: T[name][:]
        if st is None:
            return lambda T: T[name][:, a:b]
        return lambda T: T[name][:, a:b:st]

    def slide(name, k):
        return lambda T: T[name][:, 15 - k:15 - k + 128]

    nd = [0]

    def load(q, dst, src, cost):
        k = nd[0]
        nd[0] += 1
        add(q, lambda g, T: (g.sync if q == "Y" else g.scalar).dma_start(T[dst][:], T[src][:]), [], al(dst), cost, dma=k)

    load("Y", "SI", "s0", 2.5)
    load("S", "PI", "p0", 2.5)
    load("Y", "X", "x0", 6.0)
    load("S", "PLT", "pl", 6.0)
    load("Y", "L0", "z0", 6.0)
    load("Y", "THI", "th", 6.0)
    load("S", "FA", "f0", 6.0)

    def G(fn, wr, n):
        add("G", fn, [], wr, 0.15 + 2 * n * CY)
    G(lambda g, T: g.iota(T.ip[:], [[0, 1]], 0, 1), al("ip"), 1)
    G(lambda g, T: g.iota(T.irow[:], [[1, 144]], 0, 0), al("irow"), 144)
    G(lambda g, T: g.iota(T.ibase[:], [[256, 12]], 0, 0), al("ibase"), 12)
    V(ts(B("ig"), B("ip"), 4, None, A.arith_shift_right), al("ip"), al("ig"), 1)
    V(tc(B("pf"), B("ip")), al("ip"), al("pf"), 1)
    V(tc(B("gf"), B("ig")), al("ig"), al("gf"), 1)
    V(tc(B("row"), B("irow")), al("irow"), al("row"), 144)
    V(ts(B("igrow"), B("irow", 0, 128), 4, None, A.arith_shift_right), al("irow"), al("igrow"), 128)
    V(tc(B("grow"), B("igrow")), al("igrow"), al("grow"), 128)
    V(ts(B("g16"), B("gf"), 16.0, None, A.mult), al("gf"), al("g16"), 1)
    V(ts(B("g15"), B("gf"), 16.0, 15.0, A.mult, A.add), al("gf"), al("g15"), 1)
    V(ts(B("p1"), B("pf"), 1.0, None, A.add), al("pf"), al("p1"), 1)
    V(tt(B("lf"), B("pf"), B("g16"), A.subtract), al("pf", "g16"), al("lf"), 1)
    V(ts(B("l21"), B("lf"), 2.0, 1.0, A.mult, A.add), al("lf"), al("l21"), 1)
    V(ts(B("l0"), B("lf"), 0.0, None, A.is_equal), al("lf"), al("l0"), 1)
    V(ts(B("nl0"), B("l0"), -1.0, None, A.mult), al("l0"), al("nl0"), 1)
    V(ts(B("nl15"), B("lf"), 15.0, None, A.not_equal), al("lf"), al("nl15"), 1)
    V(ts(B("r16"), B("lf"), 16.0, 7.5, A.mult, A.add), al("lf"), al("r16"), 1)
    V(ts(B("base"), B("ibase"), B("r16"), None, A.add), al("ibase", "r16"), al("base"), 12)
    V(ts(B("W1"), B("row"), B("g15"), None, A.is_equal), al("row", "g15"), al("W1"), 144)
    V(ts(B("Wm"), B("row"), B("g15"), -1.0, A.is_equal, A.mult), al("row", "g15"), al("Wm"), 144)
    V(ts(B("W2"), B("row"), B("g15"), 2.0, A.is_equal, A.mult), al("row", "g15"), al("W2"), 144)
    V(ts(B("Wu"), B("row"), B("g15"), B("l21"), A.is_equal, A.mult), al("row", "g15", "l21"), al("Wu"), 144)
    V(ts(B("Wh"), B("row"), B("g15"), None, A.is_equal), al("row", "g15"), al("Wh"), 144)
    R128 = B("row", 0, 128)
    V(ts(B("Ib"), R128, B("pf"), None, A.is_equal), al("row", "pf"), al("Ib"), 128)
    V(ts(B("Ihf"), R128, B("pf"), 0.5, A.is_equal, A.mult), al("row", "pf"), al("Ihf"), 128)
    V(ts(B("I100"), R128, B("pf"), -100.0, A.is_equal, A.mult), al("row", "pf"), al("I100"), 128)
    V(ts(B("Ih"), R128, B("pf"), None, A.is_equal), al("row", "pf"), al("Ih"), 128)
    V(ts(B("OB"), B("grow"), B("gf"), None, A.is_equal), al("grow", "gf"), al("OB"), 128)
    V(ts(B("im8"), B("irow", 0, 128), NC - 1, None, A.bitwise_and), al("irow"), al("im8"), 128)
    V(ts(B("mk"), B("im8"), NC - NQ - 0.5, -1.0, A.is_lt, A.mult), al("im8"), al("mk"), 128)
    V(tt(B("OBm"), B("mk"), B("OB"), A.mult), al("mk", "OB"), al("OBm"), 128, 2)
    V(ts(B("Im"), R128, B("pf"), -1.0, A.is_equal, A.mult), al("row", "pf"), al("Im"), 128)
    V(ts(B("GT"), R128, B("pf"), None, A.is_gt), al("row", "pf"), al("GT"), 128)
    V(tt(B("Ls"), B("GT"), B("OB"), A.mult), al("GT", "OB"), al("Ls"), 128, 2)
    V(tt(B("Li"), B("Ls"), B("Ib"), A.add), al("Ls", "Ib"), al("Li"), 128, 2)
    V(ts(B("Tp"), R128, B("g16"), None, A.is_equal), al("row", "g16"), al("Tp"), 128)
    V(tt(B("TpI"), B("Tp"), B("Ih"), A.subtract), al("Tp", "Ih"), al("TpI"), 128, 2)
    V(ts(B("Sh"), R128, B("p1"), B("nl15"), A.is_equal, A.mult), al("row", "p1", "nl15"), al("Sh"), 128)
    V(tt(B("ShI"), B("Sh"), B("Ih"), A.subtract), al("Sh", "Ih"), al("ShI"), 128, 2)
    V(lambda g, T: g.vector.memset(T.zz[:], 0.0), [], al("zz"), I)
    V(lambda g, T: g.vector.memset(T.cq[:], -0.5), [], al("cq"), I)
    V(lambda g, T: g.vector.memset(T.c75[:], -7.5), [], al("c75"), 16)

    V(tc(B("PU"), B("PI")), al("PI"), al("PU"), 12)
    V(tc(B("SU"), B("SI")), al("SI"), al("SU"), I)
    V(ts(B("E16"), lambda T: T.PLT[:, :].indirect(T.PU[:, 0:12]), -CEN, None, A.add), al("PLT", "PU"), al("E16"), I, 1.6)
    V(ts(B("EU"), B("E16"), CEN, None, A.add), al("E16"), al("EU"), I)
    V(ts(B("b5", 0, I), B("SI"), -CEN, None, A.add), al("SI"), [("b5", 0, I)], I)
    V(tc(B("PF"), B("PI")), al("PI"), al("PF"), 12)
    V(tc(B("BND"), B("THI")), al("THI"), al("BND"), I)

    def gathers():
        cs = CSPL
        V(lambda g, T: g.vector.tensor_copy(T.XS[:, 0:16 * cs], T.X[:, :].indirect(T.SU[:, 0:cs])), al("X", "SU"), [("XS", 0, 16 * cs)], 16 * cs, 1.5)
        if cs < I:
            S(lambda g, T: g.scalar.activation(T.XS[:, 16 * cs:W], T.X[:, :].indirect(T.SU[:, cs:I]), F.Copy), al("X", "SU"), [("XS", 16 * cs, W)], 16 * (I - cs), 1.5)
        for c in range(XC):
            a, b = I // XC * c, I // XC * (c + 1)
            S(lambda g, T, a=a, b=b: g.scalar.activation(T.XE[:, 16 * a:16 * b], T.X[:, :].indirect(T.EU[:, a:b]), F.Copy), al("X", "EU"), [("XE", 16 * a, 16 * b)], 16 * (b - a), 1.5)

    gathers()

    def mixed(n):
        fast, slow = list(range(NC - n)), list(range(NC - n, NC))
        res = []
        while fast or slow:
            if slow and (not fast or len(slow) * (NC - n) >= len(fast) * n):
                res.append(slow.pop(0))
            else:
                res.append(fast.pop(0))
        return res

    turn_bank = [0]

    def bank():
        turn_bank[0] += 1
        return "b4" if turn_bank[0] % 2 else "b6"

    for t in range(TURNS):
        L, Y = "L%d" % t, "Y%d" % t
        f0, f1 = ("FA", "FB") if t % 2 == 0 else ("FB", "FA")
        s0, s1 = (0, I) if t % 2 == 0 else (I, 0)
        if t == 0:
            for c in range(16):
                S(act(B("IC", 128 * c, 128 * c + 128), B("Ib"), F.Copy, scale=float(c + 1)), al("Ib"), [("IC", 128 * c, 128 * c + 128)], 128)
        MM(B("b3", 0, I), B("Ib"), B("zz"), True, False, al("Ib", "zz"), [("b3", 0, I)], I)
        for c in range(XC):
            p, q = I // XC * c, I // XC * (c + 1)
            for k in [k for k in range(16) if k % NC < NC - NQ]:
                MM(B("b3", p, q), slide("Wm", k), B("XE", 16 * p + k, 16 * q, 16), False, False, al("Wm") + [("XE", 16 * p, 16 * q)], [("b3", p, q)], q - p)
        for m in range(NK):
            MM(B("b0", m, CW, NK), B("Ib"), B(L), True, True, al("Ib", L), [("b0", 0, CW)], I)
        MM(B("b3", 0, I), B("OBm"), B(L), False, False, al("OBm", L), [("b3", 0, I)], I)
        for r in range(16):
            MM(B("b7", 0, 12), slide("Wu", r), B(L, r, I, 16), r == 0, r == 15, al("Wu", L), [("b7", 0, 12)], 12)
        MM(B("b7", 256, 256 + I), B("Ihf"), B(L), True, False, al("Ihf", L), [("b7", 256, 256 + I)], I)
        MM(B("b7", 256, 256 + I), B("Ihf"), B(f0), False, False, al("Ihf", f0), [("b7", 256, 256 + I)], I)
        MM(B("b7", 256, 256 + I), B("Ihf"), B("cq"), False, True, al("Ihf", "cq"), [("b7", 256, 256 + I)], I)
        V(ts(B(f1), B("b7", 256, 256 + I), MAGIC, MAGIC, A.add, A.subtract), [("b7", 256, 256 + I)], al(f1), I)
        V(tc(B("H1"), B("b7", 0, 12)), [("b7", 0, 12)], al("H1"), 12)
        V(ts(B("H2"), B("H1"), 4095, None, A.bitwise_and), al("H1"), al("H2"), 12)
        V(ts(B("H3"), B("H2"), 1184.0, None, A.add), al("H2"), al("H3"), 12)
        V(tt(B("H4"), B("H2"), B("H3"), A.mult), al("H2", "H3"), al("H4"), 12)
        V(ts(B("H7"), B("H4"), 5, PLN - 1, A.arith_shift_right, A.bitwise_and), al("H4"), al("H7"), 12)
        V(tc(B("PU"), B("H7")), al("H7"), al("PU"), 12)
        V(ts(B("CAND"), lambda T: T.PLT[:, :].indirect(T.PU[:, 0:12]), -CEN, None, A.add), al("PLT", "PU"), al("CAND"), I, 1.6)
        V(tt(B("DES"), B("E16"), B("b5", s0, s0 + I), A.subtract), al("E16") + [("b5", s0, s0 + I)], al("DES"), I)
        def tensor_diff(X, q, bk):
            for m in range(NK):
                k = q + NC * m
                MM(B(bk, I * m, I * m + I), B("Ib"), lambda T, k=k: T[X][:, k:W:16], True, False, al("Ib", X), [(bk, I * m, I * m + I)], I)
                MM(B(bk, I * m, I * m + I), B("Im"), B(L), False, True, al("Im", L), [(bk, I * m, I * m + I)], I)

        VQ = NC - NS
        for q in range(VQ):
            V(tt(B("D", CW * q, CW * q + CW), lambda T, q=q: T.XS[:, q:W:NC], B("b0", 0, CW), A.subtract),
              al("XS") + [("b0", 0, CW)], [("D", CW * q, CW * q + CW)], CW)
        chunks = [(c, min(VQ, c + 2)) for c in range(0, VQ, 2)]
        for c, e in chunks:
            a, b = CW * c, CW * e
            S(act(B("AB", a, b), B("D", a, b), F.Abs), [("D", a, b)], [("AB", a, b)], b - a)
        for q in range(VQ, NC):
            bk = bank()
            tensor_diff("XS", q, bk)
            S(act(B("AB", CW * q, CW * q + CW), B(bk, 0, CW), F.Abs), [(bk, 0, CW)], [("AB", CW * q, CW * q + CW)], CW)
            S(act(B("SG", CW * q, CW * q + CW), B(bk, 0, CW), F.Sign, bias=-0.5), [(bk, 0, CW)], [("SG", CW * q, CW * q + CW)], CW)
        for c, e in chunks:
            a, b = CW * c, CW * e
            if c < 2 * NF:
                V(ts(B("SG", a, b), B("D", a, b), 0.0, -0.5, A.is_gt, A.add), [("D", a, b)], [("SG", a, b)], b - a, 0.5)
            else:
                S(act(B("SG", a, b), B("D", a, b), F.Sign, bias=-0.5), [("D", a, b)], [("SG", a, b)], b - a)

        def piece(buf, q, m, direct):
            return B(buf, CW * q + I * m, CW * q + I * m + I) if direct else B(buf, CW * q + m, CW * q + CW, NK)

        sq = [(q, m) for q in mixed(NS) for m in range(NK)]
        for (q, m) in sq:
            MM(B("b1", 0, I), slide("W1", q + NC * m), piece("AB", q, m, q >= VQ), (q, m) == sq[0], (q, m) == sq[-1], al("W1") + [("AB", CW * q, CW * q + CW)], [("b1", 0, I)], I)
        gq = sq if NS == 0 else [x for x in sq if x[0] >= VQ] + [x for x in sq if x[0] < VQ]
        for (q, m) in gq:
            w = "W2" if q < min(VQ, 2 * NF) else "W1"
            MM(B("b2", 0, I), slide(w, q + NC * m), piece("SG", q, m, q >= VQ), (q, m) == gq[0], (q, m) == gq[-1], al(w) + [("SG", CW * q, CW * q + CW)], [("b2", 0, I)], I)
        for q in range(NC - NQ, NC):
            bk = bank()
            tensor_diff("XE", q, bk)
            S(act(B("MX", CW * q, CW * q + CW), B(bk, 0, CW), F.Abs), [(bk, 0, CW)], [("MX", CW * q, CW * q + CW)], CW)
        for q in range(NC - NQ):
            V(tt(B("MX", CW * q, CW * q + CW), lambda T, q=q: T.XE[:, q:W:NC], B("b0", 0, CW), A.max),
              al("XE") + [("b0", 0, CW)], [("MX", CW * q, CW * q + CW)], CW)
        pq = [(q, m) for q in mixed(NQ) for m in range(NK)]
        for (q, m) in pq:
            k = q + NC * m
            if q < NC - NQ:
                MM(B("b3", 0, I), slide("W2", k), B("MX", CW * q + m, CW * q + CW, NK), False, (q, m) == pq[-1], al("W2") + [("MX", CW * q, CW * q + CW)], [("b3", 0, I)], I)
            else:
                MM(B("b3", 0, I), slide("W1", k), B("MX", CW * q + I * m, CW * q + I * m + I), False, (q, m) == pq[-1], al("W1") + [("MX", CW * q, CW * q + CW)], [("b3", 0, I)], I)
        V(tt(B("RS"), B("b1", 0, I), B("BND"), A.is_lt), [("b1", 0, I)] + al("BND"), al("RS"), I)
        MM(B("b1", I, 2 * I), B("Ls"), B("RS"), True, True, al("Ls", "RS"), [("b1", I, 2 * I)], I)
        V(tt(B("FI"), B("RS"), B("b1", I, 2 * I), A.is_gt), al("RS") + [("b1", I, 2 * I)], al("FI"), I)
        V(tt(B("FF"), B("FI"), B("b5", s0, s0 + I), A.mult), al("FI") + [("b5", s0, s0 + I)], al("FF"), I)
        MM(B("b4", I, 2 * I), B("Li"), B("RS"), True, True, al("Li", "RS"), [("b4", I, 2 * I)], I)
        S(act(B("b1", 0, I), B("b4", I, 2 * I), F.Relu, scale=-1.0, bias=1.0), [("b4", I, 2 * I)], [("b1", 0, I)], I)
        S(act(B("KK"), B("b2", 0, I), F.Relu, scale=16.0, bias=128.0), [("b2", 0, I)], al("KK"), I)
        MM(B("b2", I, 2 * I), B("OB"), B("RS"), True, False, al("OB", "RS"), [("b2", I, 2 * I)], I)
        MM(B("b2", I, 2 * I), B("I100"), B("FI"), False, True, al("I100", "FI"), [("b2", I, 2 * I)], I)
        V(tt(B("b2", 0, I), B("b2", I, 2 * I), B("KK"), A.is_gt), [("b2", I, 2 * I)] + al("KK"), [("b2", 0, I)], I)
        V(tt(B("WD"), B("DES"), B("b2", 0, I), A.mult), al("DES") + [("b2", 0, I)], al("WD"), I)
        V(tt(B("RR"), B("WD"), B("b5", s0, s0 + I), A.add), al("WD") + [("b5", s0, s0 + I)], al("RR"), I)
        V(tt(B("QQ"), B("RR"), B("b1", 0, I), A.mult), al("RR") + [("b1", 0, I)], al("QQ"), I)
        V(tt(B("RP"), B("b3", 0, I), B("BND"), A.is_lt), [("b3", 0, I)] + al("BND"), al("RP"), I)
        MM(B("b3", I, 2 * I), B("OB"), B("RS"), True, False, al("OB", "RS"), [("b3", I, 2 * I)], I)
        MM(B("b3", I, 2 * I), B("Ls"), B("RP"), False, True, al("Ls", "RP"), [("b3", I, 2 * I)], I)
        MM(B("b4", 0, I), B("OB"), B("RS"), True, False, al("OB", "RS"), [("b4", 0, I)], I)
        MM(B("b4", 0, I), B("OB"), B("RP"), False, True, al("OB", "RP"), [("b4", 0, I)], I)
        V(tt(B("b6", I, 2 * I), B("RP"), B("b3", I, 2 * I), A.is_gt), al("RP") + [("b3", I, 2 * I)], [("b6", I, 2 * I)], I)
        S(act(B("b4", I, 2 * I), B("b4", 0, I), F.Relu, scale=B("nl0"), bias=B("l0")), [("b4", 0, I)] + al("nl0", "l0"), [("b4", I, 2 * I)], I)
        V(tt(B("b6", 0, I), B("E16"), B("b6", I, 2 * I), A.mult), al("E16") + [("b6", I, 2 * I)], [("b6", 0, I)], I)
        V(tt(B("HH"), B("CAND"), B("b4", I, 2 * I), A.mult), al("CAND") + [("b4", I, 2 * I)], al("HH"), I)
        V(tt(B("GG"), B("HH"), B("b6", 0, I), A.add), al("HH") + [("b6", 0, I)], al("GG"), I)
        for src in ("FF", "GG"):
            for r in range(16):
                MM(B("b7", 16, 28), slide("Wh", r), B(src, r, I, 16), (src, r) == ("FF", 0), (src, r) == ("GG", 15), al("Wh", src), [("b7", 16, 28)], 12)
        V(ts(B("TU"), B("b7", 16, 28), CEN, None, A.add), [("b7", 16, 28)], al("TU"), 12)
        V(lambda g, T, f1=f1: g.vector.tensor_tensor(T.YD[:], T.X[:, :].indirect(T.TU[:, 0:12]), T[f1][:], A.subtract), al("X", "TU", f1), al("YD"), I, 1.6)
        S(act(B(Y), B("YD"), F.Abs), al("YD"), al(Y), I)
        if t < TURNS - 1:
            add("G", ("send", t), al(Y), [], 1.2, send=t)
            Ln = "L%d" % (t + 1)
            bl = (-t) % N
            a, b = BLK * bl, BLK * bl + BLK
            S(act(B(Ln, a, b), B(Y, a, b), F.Copy), al(Y), [(Ln, a, b)], BLK)
            wr = [(Ln, c, d) for c, d in ((0, a), (b, I)) if d > c]
            add("R", None, [], wr, 3.8, arr=t)
        MM(B("b7", 32, 44), B("Ib"), B("c75", 0, 12), True, False, al("Ib", "c75"), [("b7", 32, 44)], 12)
        for r in range(16):
            MM(B("b7", 32, 44), slide("W1", r), B(Y, r, I, 16), False, r == 15, al("W1", Y), [("b7", 32, 44)], 12)
        MM(B("b0", 0, I), B("Ihf"), B(L), True, False, al("Ihf", L), [("b0", 0, I)], I)
        MM(B("b0", 0, I), B("Ihf"), B("cq"), False, False, al("Ihf", "cq"), [("b0", 0, I)], I)
        MM(B("b0", 0, I), B("Ihf"), B(Y), False, True, al("Ihf", Y), [("b0", 0, I)], I)
        V(ts(B("QF"), B("b7", 32, 44), MAGIC16, MAGIC16, A.add, A.subtract), [("b7", 32, 44)], al("QF"), 12)
        V(tt(B("RF"), B("base"), B("b7", 32, 44), A.add), al("base") + [("b7", 32, 44)], al("RF"), 12)
        V(tt(B("MF"), B("RF"), B("QF"), A.subtract), al("RF", "QF"), al("MF"), 12)
        V(tc(B("MU"), B("MF")), al("MF"), al("MU"), 12)
        V(ts(B("WR"), B("b0", 0, I), MAGIC, MAGIC, A.add, A.subtract), [("b0", 0, I)], al("WR"), I)
        V(lambda g, T: g.vector.tensor_copy(T.X[:, :].indirect(T.MU[:, 0:12]), T.WR[:]), al("WR", "MU", "X"), al("X"), I, 3.5)
        o = (B("b5", s1, s1 + I), [("b5", s1, s1 + I)])
        MM(o[0], B("Ih"), B("RR"), True, False, al("Ih", "RR"), o[1], I)
        MM(o[0], B("ShI"), B("QQ"), False, False, al("ShI", "QQ"), o[1], I)
        MM(o[0], B("TpI"), B("FF"), False, False, al("TpI", "FF"), o[1], I)
        MM(o[0], B("Tp"), B("GG"), False, True, al("Tp", "GG"), o[1], I)
        last = t == TURNS - 1
        if last:
            V(ts(B("OS"), o[0], CEN, None, A.add), o[1], al("OS"), I)
        else:
            V(ts(B("SU"), o[0], CEN, None, A.add), o[1], al("SU"), I)
        S(act(B("CR"), B("b4", 0, I), F.Relu, scale=B("nl0"), bias=B("l0")), [("b4", 0, I)] + al("nl0", "l0"), al("CR"), I)
        S(act(B("C64"), B("b4", 0, I), F.Relu, scale=-64.0, bias=64.0), [("b4", 0, I)], al("C64"), I)
        if not last:
            S(act(B("b3", 0, I), B("b4", 0, I), F.Relu, scale=-1.0, bias=1.0), [("b4", 0, I)], [("b3", 0, I)], I)
            S(act(B("b3", I, 2 * I), B("b4", 0, I), F.Sign), [("b4", 0, I)], [("b3", I, 2 * I)], I)
            V(tt(B("b6", 0, I), B("E16"), B("b3", I, 2 * I), A.mult), al("E16") + [("b3", I, 2 * I)], [("b6", 0, I)], I)
            V(tt(B("HF"), B("CAND"), B("b3", 0, I), A.mult), al("CAND") + [("b3", 0, I)], al("HF"), I)
            V(tt(B("E16"), B("HF"), B("b6", 0, I), A.add), al("HF") + [("b6", 0, I)], al("E16"), I)
            V(ts(B("EU"), B("E16"), CEN, None, A.add), al("E16"), al("EU"), I, 0.5)
        V(tt(B("BND"), B("BND"), B("C64"), A.add), al("BND", "C64"), al("BND"), I, 2)
        if not last:
            gathers()
        for r in range(16):
            MM(B("b2", 384, 396), slide("W1", r), B("CR", r, I, 16), r == 0, r == 15, al("W1", "CR"), [("b2", 384, 396)], 12)
        V(tt(B("DP"), B("H7"), B("PF"), A.subtract), al("H7", "PF"), al("DP"), 12)
        V(tt(B("DQ"), B("DP"), B("b2", 384, 396), A.mult), al("DP") + [("b2", 384, 396)], al("DQ"), 12)
        V(tt(B("PF"), B("PF"), B("DQ"), A.add), al("PF", "DQ"), al("PF"), 12)
        if last:
            V(tt(B("CR"), B("BND"), B("THI"), A.subtract), al("BND", "THI"), al("CR"), I, 2)
            for r in range(16):
                MM(B("b2", 384, 396), slide("W1", r), B("CR", r, I, 16), r == 0, r == 15, al("W1", "CR"), [("b2", 384, 396)], 12)
            def store(dst, src):
                k = nd[0]
                nd[0] += 1
                add("Y", lambda g, T: g.sync.dma_start(T[dst][:], T[src][:]), al(src), [], 2.5, dma=k)
            store("yf", f1)
            store("ys", "OS")
            V(ts(B("MF"), B("b2", 384, 396), PLN / 1024.0, None, A.mult), [("b2", 384, 396)], al("MF"), 12)
            V(tt(B("YPF"), B("MF"), B("PF"), A.add), al("MF", "PF"), al("YPF"), 12)
            store("yp", "YPF")
            for c in range(16):
                MM(B("b0", 0, I), B("IC", 128 * c, 128 * c + 128), B("X", c, W, 16), c == 0, c == 15, [("IC", 128 * c, 128 * c + 128), ("X",)], [("b0", 0, I)], I)
            S(act(B("OX"), B("b0", 0, I), F.Copy), [("b0", 0, I)], al("OX"), I)
            store("yx", "OX")
    return ops


def _deps(ops):
    data, order = [], []
    acc = {}
    banks = {}
    sends = {}
    for i, (q, fn, rd, wr, cost, kw) in enumerate(ops):
        dd, oo = set(), set()
        seen = {}
        for lst, w in ((rd, False), (wr, True)):
            for (n, a, b) in lst:
                if n[0] == "b" and n[1:].isdigit():
                    e = seen.get(n)
                    if e is None:
                        e = banks.setdefault(n, {"q": q, "cur": [], "prev": []})
                        if e["q"] != q:
                            e["prev"], e["cur"], e["q"] = [x[0] for x in e["cur"]], [], q
                        seen[n] = e
                        dd.update(e["prev"])
                    if q == "T":
                        if e["cur"] and e["cur"][-1][0] != i:
                            oo.add(e["cur"][-1][0])
                    else:
                        for (j, c, d, w2) in e["cur"]:
                            if j != i and (w or w2) and c < b and a < d:
                                dd.add(j)
                    e["cur"].append((i, a, b, w))
                else:
                    l = acc.setdefault(n, [])
                    for (j, c, d, w2) in l:
                        if j != i and (w or w2) and c < b and a < d:
                            dd.add(j)
        for lst, w in ((rd, False), (wr, True)):
            for (n, a, b) in lst:
                if n[0] == "b" and n[1:].isdigit():
                    continue
                l = acc[n]
                if w:
                    l[:] = [x for x in l if not (a <= x[1] and x[2] <= b and x[0] != i)]
                l.append((i, a, b, w))
        if "send" in kw:
            sends[kw["send"]] = i
        if "arr" in kw:
            oo.add(sends[kw["arr"]])
        dd.discard(i)
        oo -= dd
        data.append(sorted(dd))
        order.append(sorted(oo))
    return data, order


def _schedule(ops, data, order):
    n = len(ops)
    succ = [[] for _ in range(n)]
    for i in range(n):
        for j in data[i] + order[i]:
            succ[j].append(i)
    prio = [0.0] * n
    for i in range(n - 1, -1, -1):
        prio[i] = ops[i][4] + max([prio[k] + LAT for k in succ[i]], default=0.0)
    base = list(prio)
    for i in range(n):
        if ops[i][3]:
            w = ops[i][3][0]
            prio[i] = base[i] + BONUS.get("%s:%s:%d" % (ops[i][0], w[0], w[1]), 0.0)
    left = [len(data[i]) + len(order[i]) for i in range(n)]
    ready = [0.0] * n
    pool = {}
    free = {}
    for i in range(n):
        if left[i] == 0:
            pool.setdefault(ops[i][0], []).append(i)
    out = []
    while True:
        best = None
        for q, l in pool.items():
            if not l:
                continue
            st = max(free.get(q, 0.0), min(ready[i] for i in l))
            if best is None or st < best[0]:
                best = (st, q)
        if best is None:
            break
        st, q = best
        i = max((i for i in pool[q] if ready[i] <= st + 1e-9), key=lambda i: (prio[i], -i))
        if ops[i][4] > 0.3:
            i = max((k for k in pool[q] if ready[k] <= st + HOLD), key=lambda i: (prio[i], -i))
            st = max(st, ready[i])
        pool[q].remove(i)
        dma = "dma" in ops[i][5] or q == "R"
        fin = st + ops[i][4]
        free[q] = st + (0.1 if dma else ops[i][4])
        out.append((i, st, fin))
        for k in succ[i]:
            same = ops[k][0] == q and i in order[k]
            ready[k] = max(ready[k], fin if same else fin + LAT)
            left[k] -= 1
            if left[k] == 0:
                pool.setdefault(ops[k][0], []).append(k)
    return out


_PLAN = {}


def _plan():
    if not _PLAN:
        ops = _build()
        data, order = _deps(ops)
        _PLAN["ops"], _PLAN["data"], _PLAN["sched"] = ops, data, _schedule(ops, data, order)
    return _PLAN["ops"], _PLAN["data"], _PLAN["sched"]


def rank_program(g, core, T, topo):
    rank = T.rank_of(core)
    if rank is None:
        return
    ops, data, sched = _plan()
    eng = {"V": g.vector, "S": g.scalar, "T": g.tensor, "G": g, "Y": g.sync}
    seq, cnt, clock = {}, {}, {}
    know = {q: {} for q in eng}

    def send(t):
        tr = []
        used = 0
        for b in range(N):
            to = (rank + b + t) % N
            if to == rank:
                continue
            dst = T.cores[to]
            rid, pnc = topo.addr(dst)[:2]
            e = topo.engines(core, dst)
            tr.append(RemoteDMATransfer(dst_ids=[DstId(rid=rid, pnc=pnc)], dma_engine_mask=1 << e[used % len(e)], remote_sem=T.sem["arr%d" % t],
                                        src=T["Y%d" % t][:, BLK * b:BLK * b + BLK], dst=T["L%d" % (t + 1)][:, BLK * b:BLK * b + BLK]))
            used += 1
        g.remote_dma_fused(tr, local_sem=T.sem.sent)
        return used

    sent = 0
    dmas = []
    for (i, st, fin) in sched:
        q, fn, rd, wr, cost, kw = ops[i]
        if q == "R":
            seq[i] = ("arr%d" % kw["arr"], N - 1)
            clock[i] = {}
            continue
        kn = know[q]
        need = {}
        before = [j for j in data[i] if "send" not in ops[j][5]]
        for j in before:
            s, v = seq[j]
            if kn.get(s, 0) < v:
                need[s] = max(need.get(s, 0), v)
        for j in sorted(before, key=lambda j: -j):
            s, v = seq[j]
            if s in need and need[s] == v:
                for s2, v2 in clock[j].items():
                    if s2 in need and s2 != s and need[s2] <= v2:
                        del need[s2]
        for j in before:
            s, v = seq[j]
            for s2, v2 in list(clock[j].items()) + [(s, v)]:
                if kn.get(s2, 0) < v2:
                    kn[s2] = v2
        for s, v in need.items():
            eng[q].wait_ge(T.sem[s], v)
        if "send" in kw:
            sent += send(kw["send"])
            continue
        ins = fn(g, T)
        if "dma" in kw:
            s = "dm%d" % kw["dma"]
            ins.then_inc(T.sem[s], 16)
            seq[i] = (s, 16)
            dmas.append(s)
            clock[i] = dict(kn)
        else:
            s = "q" + q
            cnt[s] = cnt.get(s, 0) + 1
            ins.then_inc(T.sem[s], 1)
            seq[i] = (s, cnt[s])
            clock[i] = dict(kn)
    g.wait_ge(T.sem.sent, sent)
    for s, v in cnt.items():
        g.wait_ge(T.sem[s], v)
    for s in dmas:
        g.wait_ge(T.sem[s], 16)
